import numpy as np, ml_dtypes
CORES = [6,15,38,47]
N = 4
import mx_ref
BF = ml_dtypes.bfloat16
def gentries(a):
    return np.ascontiguousarray(a.reshape(8, 16, -1).transpose(0, 2, 1)).reshape(8, -1)
def gtable(e):
    e = np.asarray(e); return np.ascontiguousarray(e.reshape(8, -1, 16).transpose(0, 2, 1)).reshape(128, -1).astype(np.int32)
def gcols(t, e):
    v = np.concatenate([t.reshape(8, 16, -1, 4), np.zeros((8, 16, 1, 4), BF)], axis=2)
    return np.ascontiguousarray(np.stack([v[g][:, e[g]] for g in range(8)])).reshape(128, -1)
def tile(rs):
    return np.stack(rs, axis=2).reshape(128, -1).astype(BF)
def pick(q, e):
    c = np.concatenate([q[0].reshape(128, -1, 4), np.zeros((128, 1, 4), np.uint8)], axis=1); s = np.concatenate([q[1], np.ones((16, 1), np.uint8)], axis=1)
    return (np.ascontiguousarray(c[:, e].reshape(128, -1)), np.ascontiguousarray(s[:, e]))
def join(*qs):
    return (np.concatenate([q[0] for q in qs], axis=1), np.concatenate([q[1] for q in qs], axis=1))
def put(q, e, v):
    c, s = q[0].reshape(128, -1, 4).copy(), q[1].copy(); c[:, e] = v[0].reshape(128, -1, 4); s[:, e] = v[1]
    return (c.reshape(128, -1), s)
def pk(c, s):
    return (np.ascontiguousarray(c), mx_ref.live(s))
def emit(q):
    return q[0], q[1]
def packed(v, rng):
    q = [mx_ref.quantize(np.ascontiguousarray(v[r])) for r in range(N)]
    return np.stack([a for a, b in q]), np.stack([mx_ref.plane(b, rng) for a, b in q])
def values_of_codes():
    e, c = np.zeros((128, 128, 4), np.float32), np.zeros((128, 2, 4), np.uint8)
    e[np.arange(128), np.arange(128), 0] = 1
    c[:127, :, 0] = np.arange(256).reshape(2, 128).T[:127]
    return mx_ref.matmul(mx_ref.quantize(e.reshape(128, 512).astype(BF)), (c.reshape(128, 8), np.full((16, 2), 127, np.uint8))).T.reshape(-1).astype(np.float64)
CODE_VALUE, SCALE_VALUE = values_of_codes(), 2.0 ** (np.arange(256) - 127.0)
def decode(q):
    return (CODE_VALUE[q[0]].reshape(16, 8, -1, 4) * SCALE_VALUE[q[1]][:, None, :, None] + 0.0).reshape(128, -1).astype(np.float32)
def f(rng, *shape):
    return mx_ref.flush((rng.standard_normal(shape, dtype=np.float32) * np.exp2(rng.integers(-2, 3, shape[:-1] + (1,)))).astype(BF))
def wide(rng, *shape, cols=0):
    v = rng.standard_normal(shape, dtype=np.float32) * np.exp2(rng.integers(-12, 13, shape)).astype(np.float32)
    if cols: v *= np.repeat(np.exp2(rng.integers(-cols, cols + 1, shape[:-2] + (1, shape[-1] // 4))) * (rng.random(shape[:-2] + (1, shape[-1] // 4)) > 0.0625), 4, axis=-1).astype(np.float32)
    return mx_ref.flush(v.astype(BF))
C = 448
STEP = [1, 2, 3]
def numbers_of(rng):
    return {"x": np.array(f(rng, N, 128, 4 * C)), "u": np.array(f(rng, N, 128, 512)), "v": np.array(f(rng, N, 128, 512))}
def stored(a, b):
    return {"lam": np.stack([gtable(a[r]) for r in range(N)]), "rho": np.stack([gtable(b[r]) for r in range(N)])}
def dealt(rng):
    e = np.tile(np.arange(C), (N, 8, 1))
    return np.stack([rng.permuted(e, axis=2), rng.permuted(e, axis=2)], axis=3).reshape(N, 8, 2 * C)
def lists(rng):
    a = dealt(rng)
    return stored(a, dealt(rng))
def layers(rng):
    return np.array(f(rng, N, 128, 2048)).reshape(N, 8, 16, 4, 8, 16, 4)
def weights(rng, w):
    c, p = packed(np.ascontiguousarray(w).reshape(N, 128, 2048), rng)
    return {"wc": c, "ws": p}
def unread(u):
    u = u.reshape(N, 128, 128, 4)
    u[:, :, ::16] = 0
    u[:, :, 1::16] = 0
    return u
def setup_inputs(rng):
    return {**numbers_of(rng), **lists(rng), **weights(rng, layers(rng))}
def setup_inputs_ties(rng):
    d = numbers_of(rng)
    o = rng.permutation(N)
    s = rng.integers(-1, 2, (N, 8, 2, C)).astype(np.float32)
    s[o[1]] = 1
    s[o[2]] = -1
    x = d["x"].reshape(N, 8, 16, C, 4)
    x[:, :, :2] = 0
    x[:, :, :2, :, 0] = s.astype(BF)
    c = np.ones(N, np.float32)
    c[o[0]] = 0
    u = unread(d["u"])
    for h in range(0, 128, 16):
        for i in range(2): u[:, h + i, h + i, 0] = c.astype(BF)
    w = layers(rng)
    w[:, :, :, :, :, :8] = 0
    for g in range(8): w[:, g, 15, 0, g, 15, 0] = 2.0 ** 8
    return {"x": x.reshape(N, 128, 4 * C), "u": u.reshape(N, 128, 512), "v": d["v"], **lists(rng), **weights(rng, w)}
def setup_inputs_near(rng):
    d = numbers_of(rng)
    lo = np.unique(np.minimum(np.arange(N), np.arange(N) ^ STEP[0]))
    o = np.zeros(N, np.int64)
    o[lo] = rng.permutation(N // 2) % 2
    o[lo ^ STEP[0]] = o[lo]
    k = np.where(o == 0, 2.0 ** -30, 1.0).astype(np.float32)
    some = rng.permutation(8)[:4]
    x = d["x"].astype(np.float32).reshape(N, 8, 16, C, 4)
    x[:, :, :8] = 0
    x[:, some, 8:] = 0
    for g in some: x[:, g, 15, :, 0] = k[:, None]
    for i in range(2):
        s = rng.integers(-1, 2, (N, 8, C)) * k[:, None, None]
        x[:, :, 2 * i, :, 0] = 1.125 * s
        x[:, :, 2 * i + 1, :, 0] = -1.25 * s
        x[:, :, 6, :, i] = rng.choice([-1.0, 1.0], (N, 8, C)) * k[:, None, None]
        x[:, :, 6, :, 2 + i] = rng.choice([-1.0, 1.0], (N, 8, C)) * k[:, None, None]
    x[:, :, 7, :, 0] = k[:, None, None]
    for r in range(N):
        for g in rng.permutation(8)[:4]: x[r, g, 2 * rng.integers(2), rng.integers(C), 0] = 2.0 ** 30 * rng.choice([-1.0, 1.0])
    u = unread(d["u"])
    for h in range(0, 128, 16):
        for i in range(2):
            u[:, h + 2 * i, h + i, 0] = (1.125 * k).astype(BF)
            u[:, h + 2 * i + 1, h + i, 0] = k.astype(BF)
            u[:, h + 4 + i, h + i, 0] = k.astype(BF)
    w = layers(rng)
    w[:, :, :8] = 0
    w[:, :, :, :, :, :8] = 0
    w[:, :8] = 0
    for g in range(8):
        for i in range(2): w[:, g, 6, 0, g, 4 + i, i] = 2.0 ** -8
        w[:, g, 7, 0, g, 7, 0] = 32.0
    for g in some:
        for i in range(2):
            u[:, 16 * g + 8 + 2 * i, 16 * g + i, 0] = (1.125 * k).astype(BF)
            u[:, 16 * g + 9 + 2 * i, 16 * g + i, 0] = k.astype(BF)
            w[:, g, 6, 0, g, 8 + 2 * i, 2 + i] = 1.125 * 2.0 ** -8
            w[:, g, 6, 0, g, 9 + 2 * i, 2 + i] = -1.25 * 2.0 ** -8
        w[:, g, 7, 0, g, 14, 0] = 32.0
    return {"x": x.reshape(N, 128, 4 * C).astype(BF), "u": u.reshape(N, 128, 512), "v": d["v"], **lists(rng), **weights(rng, w)}
def setup_inputs_odd(rng):
    d = numbers_of(rng)
    x = d["x"].astype(np.float32).reshape(N, 8, 16, C, 4)
    x[:, :, 8:] = 0
    x[:, :, 0, :, 0] = 1.96875 * 2.0 ** 8
    for i in range(2):
        x[:, :, 1 + 2 * i, :, 0] = 2.0 ** -5
        x[:, :, 2 + 2 * i, :, 0] = (7 + 2 * rng.integers(0, 2, (N, 8, C))) * 2.0 ** -8
    x[:, :, 8, :, 0] = -1.125
    x[:, :, 10, :, 0] = 0.0703125 * rng.choice([-1.0, 1.0], (N, 8, C))
    u = unread(d["u"])
    for h in range(0, 128, 16):
        for i in range(2):
            c = rng.choice([-1.0, 1.0], N).astype(np.float32)
            u[:, h + 1 + 2 * i, h + i, 0] = c.astype(BF)
            u[:, h + 2 + 2 * i, h + i, 0] = (-1.125 * c).astype(BF)
    w = np.zeros((N, 8, 16, 4, 8, 16, 4), np.float32)
    for g in range(8):
        w[:, g, 8, 0, g, 8, 0] = -28.0
        w[:, g, 2, 0, g, 12, 0] = 32.0
        for b in range(4): w[:, g, 10, b, g, 9, 0] = -2.0 ** (b - 5)
    return {"x": x.reshape(N, 128, 4 * C).astype(BF), "u": u.reshape(N, 128, 512), "v": d["v"], **lists(rng), **weights(rng, w.astype(BF))}
def setup_inputs_ends(rng):
    d = numbers_of(rng)
    o, e = rng.permutation(N) % 4, rng.permutation(N) % 4
    s = rng.choice([-1.0, 1.0], (N, 128, C, 4))
    s[o == 0] = -1
    s[o == 1] = rng.choice([-1.0, 1.0], (N, 1, C, 1))[o == 1]
    x = s * (0.93 + 0.02 * rng.random((N, 128, C, 4))) * 2.0 ** 30
    x[o == 3] = 2.0 ** -30
    size = np.where(o == 3, 2.0 ** -30, 2.0 ** 30)
    u = unread(d["u"])
    for r in range(N):
        h = rng.permutation(8)
        for i in range(2):
            c = np.where(h < 2, 0.0, ((h >> i) % 2) * 2.0 - 1.0) * size[r]
            u[r, :, i::16] = c.astype(np.float32).astype(BF)[None, :, None]
    v = rng.choice([-1.0, 1.0], (N, 128, 512)) * np.where(o < 2, 2.0 ** 30, 2.0 ** -30)[:, None, None]
    t = rng.integers(0, C, (2, N, 8, 2 * C))
    t[:, e == 0] = C - 1
    t[:, e == 1] = 0
    t[:, e == 2] = np.arange(2 * C) % 2 * (C - 1)
    w = np.zeros((N, 128, 4, 128, 4), np.float32)
    j = np.arange(127)
    for b in range(4): w[:, j, b, j, b] = np.array([-0.25, -0.25, -2.0 ** -8, 32.0])[o][:, None]
    return {"x": x.astype(np.float32).reshape(N, 128, 4 * C).astype(BF), "u": u.reshape(N, 128, 512), "v": v.astype(np.float32).astype(BF), **stored(t[0], t[1]), **weights(rng, w.astype(BF))}
def setup_inputs_spread(rng):
    d = setup_inputs(rng)
    d["x"] = wide(rng, N, 128, 4 * C, cols=6)
    return d
def check_inputs(d):
    b = []
    for k in ("x", "u", "v"):
        a = np.abs(d[k].astype(np.float32))
        if not (np.isfinite(a).all() and ((a == 0) | (a >= 2.0 ** -30) & (a <= 2.0 ** 30)).all()): b.append("a value of " + k)
    for k in ("lam", "rho"):
        if not ((d[k] >= 0) & (d[k] < C)).all(): b.append("an entry of " + k)
    none, least, most = [emit(mx_ref.quantize(np.full((128, 16), k, np.float32).astype(BF)))[1][0, 0] for k in (0.0, 2.0 ** -8, 2.0 ** 8)]
    for r in range(N):
        if ((d["wc"][r] == 0x7F) | (d["wc"][r] == 0xFF)).any(): b.append("wc: a code that is no number")
        s = mx_ref.live(d["ws"][r])
        if ((s != none) & ((s < least) | (s > most))).any(): b.append("ws: a scale out of range")
        if (((d["wc"][r].reshape(16, 8, 512, 4) & 0x7F) != 0) & (s == none)[:, None, :, None]).any(): b.append("wc: a code other than zero under the scale of zeros")
    return b
def swapped(t, where):
    a = t.reshape(8, C, 2)
    return np.where(where[:, :, None], a[:, :, ::-1], a).reshape(8, 2 * C)
def reference(x, u, v, lam, rho, wc, ws):
    qu = [mx_ref.quantize(u[r]) for r in range(N)]
    lay = [pk(wc[r], ws[r]) for r in range(N)]
    left, right = [gentries(lam[r]) for r in range(N)], [gentries(rho[r]) for r in range(N)]
    now = [x[r] for r in range(N)]
    q = [mx_ref.quantize(now[r]) for r in range(N)]
    s = [mx_ref.matmul(qu[r], q[r]) for r in range(N)]
    for step in STEP:
        at, mid, sent = [], [], []
        for r in range(N):
            bit = (s[r][::16] > 0).astype(np.int64)
            up, down = np.zeros((8, C), np.int64), np.zeros((8, C), np.int64)
            up[0] = np.arange(C)
            down[7] = np.arange(C)
            for g in range(7):
                up[g + 1] = left[r][g][2 * up[g] + bit[g]]
            for g in range(7, 0, -1):
                down[g - 1] = right[r][g][2 * down[g] + bit[g]]
            at.append(np.take_along_axis(up, down, axis=1))
            mid.append(((now[r].astype(np.float32) + gcols(now[r], at[r]).astype(np.float32)) * np.float32(0.5)).astype(BF))
            z = mx_ref.quantize(mid[r])
            sent.append(mx_ref.quantize(tile([mx_ref.matmul(pick(lay[r], np.arange(128 * b, 128 * b + 128)), z) * np.float32(0.03125) for b in range(4)])))
        for r in range(N):
            p = r ^ step
            far = gcols(decode(sent[p]).astype(BF), np.take_along_axis(at[p], at[r], axis=1))
            now[r] = (mid[r].astype(np.float32) + far.astype(np.float32)).astype(BF)
            q[r] = mx_ref.quantize(now[r])
            s[r] = mx_ref.matmul(qu[r], q[r])
            left[r], right[r] = swapped(left[r], s[r][1::16] < 0), swapped(right[r], s[r][1::16] > 0)
    y, lr = np.zeros((N, 128, C), np.float32), np.zeros((N, 8, 4 * C), np.float32)
    oc, osc = np.zeros((N, 128, 4 * C), np.uint8), np.zeros((N, 16, C), np.uint8)
    for r in range(N):
        y[r] = mx_ref.matmul(mx_ref.quantize(v[r]), q[r])
        lr[r] = np.concatenate([left[r], right[r]], axis=1)
        oc[r], osc[r] = emit(q[r])
    return {"y": y, "lr": lr, "oc": oc, "osc": osc}

@@ -1,0 +1,467 @@
+import numpy as np
+from concourse.mybir import dt, AluOpType, ActivationFunctionType
+
+C = 448
+STEP = [1, 2, 3]
+PIECES = [(0, 256), (256, 448)]
+HALVES = [(0, 8), (8, 14)]
+TINY = 2.0 ** -100
+
+SCRATCH = {
+    "ut": ("sbuf", [128, 512], "bfloat16"), "vt": ("sbuf", [128, 512], "bfloat16"),
+    "uq": ("sbuf", [128, 128], "float8_e4m3fn_x4"), "us": ("sbuf", [128, 128], "uint8"),
+    "vvq": ("sbuf", [128, 128], "float8_e4m3fn_x4"), "vvs": ("sbuf", [128, 128], "uint8"),
+    "ubq": ("sbuf", [128, 128], "float8_e4m3fn_x4"), "ubs": ("sbuf", [128, 128], "uint8"),
+    "ufq": ("sbuf", [128, 128], "float8_e4m3fn_x4"), "ufs": ("sbuf", [128, 128], "uint8"),
+    "wq": ("sbuf", [128, 512], "float8_e4m3fn_x4"), "wsp": ("sbuf", [128, 512], "uint8"),
+    "raw": ("sbuf", [128, 896], "int32"), "ident": ("sbuf", [128, 896], "int32"),
+    "pi": ("sbuf", [128, 1], "int32"), "pi2": ("sbuf", [128, 8], "int32"),
+    "a2": ("sbuf", [128, 8], "float32"), "cc": ("sbuf", [128, 32], "float32"),
+    "gr": ("sbuf", [128, 128], "float32"),
+    "ce": ("sbuf", [128, 14], "float32"), "co": ("sbuf", [128, 14], "float32"),
+    "lef": ("sbuf", [128, 14], "float32"), "lof": ("sbuf", [128, 14], "float32"),
+    "le": ("sbuf", [128, 14], "uint16"), "lo": ("sbuf", [128, 14], "uint16"),
+    "lb": ("sbuf", [128, 8], "uint16"), "lf": ("sbuf", [128, 8], "uint16"),
+    "ones": ("sbuf", [128, 512], "bfloat16"),
+    "eo": ("sbuf", [128, 896], "float32"), "mt": ("sbuf", [128, 448], "float32"), "dtb": ("sbuf", [128, 448], "float32"),
+    "mm": ("sbuf", [128, 448], "float32"), "dd": ("sbuf", [128, 448], "float32"), "lrb": ("sbuf", [128, 896], "float32"),
+    "phi": ("sbuf", [128, 448], "float32"), "beta": ("sbuf", [128, 448], "float32"),
+    "be": ("sbuf", [128, 224], "float32"), "bo": ("sbuf", [128, 224], "float32"),
+    "tbo": ("sbuf", [128, 224], "float32"),
+    "ie": ("sbuf", [128, 14], "float32"), "cl": ("sbuf", [128, 224], "float32"), "labe": ("sbuf", [128, 224], "float32"),
+    "be2": ("sbuf", [128, 224], "float32"), "mlf": ("sbuf", [128, 28], "float32"),
+    "kp": ("sbuf", [128, 28], "uint16"), "ml2": ("sbuf", [128, 28], "uint16"), "kk": ("sbuf", [128, 28], "uint16"),
+    "pr2": ("sbuf", [128, 896], "float32"), "rw2": ("sbuf", [128, 896], "float32"),
+    "gk2": ("sbuf", [128, 448], "float32"), "tk2": ("sbuf", [128, 448], "float32"),
+    "ml": ("sbuf", [128, 28], "uint16"), "kn": ("sbuf", [128, 28], "uint16"),
+    "pr": ("sbuf", [128, 896], "float32"), "rw": ("sbuf", [128, 896], "float32"),
+    "gk": ("sbuf", [128, 448], "float32"), "tk": ("sbuf", [128, 448], "float32"),
+    "xj": ("sbuf", [128, 4 * C], "bfloat16"), "vm": ("sbuf", [128, 4 * C], "bfloat16"), "vq": ("sbuf", [128, C], "float8_e4m3fn_x4"), "vs": ("sbuf", [128, C], "uint8"),
+    "hl": ("sbuf", [128, 4 * C], "bfloat16"), "yb": ("sbuf", [128, C], "float32"),
+    "ps": ("psum", [128, 4096], "float32"),
+}
+for _t in range(8):
+    SCRATCH["o%d" % (_t % 2)] = ("sbuf", [128, 224], "float32")
+    SCRATCH["t%d" % (_t % 2)] = ("sbuf", [128, 224], "float32")
+    SCRATCH["of%d" % _t] = ("sbuf", [128, 14], "uint16")
+for _b in range(4):
+    SCRATCH["xh%d" % _b] = ("sbuf", [128, C], "bfloat16")
+    SCRATCH["d%d" % _b] = ("sbuf", [128, C], "bfloat16")
+    SCRATCH["et%d" % _b] = ("sbuf", [128, 512], "bfloat16")
+    SCRATCH["eq%d" % _b] = ("sbuf", [128, 128], "float8_e4m3fn_x4")
+    SCRATCH["es%d" % _b] = ("sbuf", [128, 128], "uint8")
+for _r in range(4):
+    SCRATCH["x%d" % _r] = ("sbuf", [128, 4 * C], "bfloat16")
+    SCRATCH["xq%d" % _r] = ("sbuf", [128, C], "float8_e4m3fn_x4")
+    SCRATCH["xs%d" % _r] = ("sbuf", [128, C], "uint8")
+for _r in range(3):
+    SCRATCH["kx%d" % _r] = ("sbuf", [128, 28], "uint16")
+    SCRATCH["lk%d" % _r] = ("sbuf", [128, 28], "uint16")
+    SCRATCH["hq%d" % _r] = ("sbuf", [128, C], "float8_e4m3fn_x4")
+    SCRATCH["hs%d" % _r] = ("sbuf", [128, C], "uint8")
+    SCRATCH["lq%d" % _r] = ("sbuf", [128, C], "float8_e4m3fn_x4")
+    SCRATCH["ls%d" % _r] = ("sbuf", [128, C], "uint8")
+
+SEMAPHORES = ["sv", "ss", "st", "sg", "lx0", "lx1", "lu", "ltab", "lid", "lw", "lv", "sent", "outs"] + ["arr%d%d" % (r, k) for r in range(3) for k in range(2)] + ["ka%d" % r for r in range(3)] + ["sw%d" % r for r in range(3)]
+
+
+def flow(g, T):
+    Q = {"v": g.vector, "s": g.scalar, "t": g.tensor, "g": g, "y": g.sync}
+    own = {"v": "sv", "s": "ss", "t": "st", "g": "sg"}
+    count = {}
+    clock = {q: {} for q in Q}
+    log = {}
+    order = [0]
+
+    def meet(a, b):
+        return a[1] < b[2] and b[1] < a[2] and a[3] < b[4] and b[3] < a[4] and not (a[5] == b[5] and a[6] != b[6])
+
+    def inside(a, b):
+        return a[1] <= b[1] and b[2] <= a[2] and a[3] <= b[3] and b[4] <= a[4] and (a[5] == 1 or (a[5] == b[5] and a[6] == b[6]))
+
+    def know(q, rec):
+        for s, n in rec[5].items():
+            if clock[q].get(s, 0) < n:
+                clock[q][s] = n
+
+    def settle(q, reads, writes, dma):
+        need = []
+        for reg in reads:
+            for rec in log.get(reg[0], []):
+                if rec[1] and meet(reg, rec[0]):
+                    need.append(rec)
+        for reg in writes:
+            for rec in log.get(reg[0], []):
+                if meet(reg, rec[0]) and not (not rec[1] and rec[4] == q and not dma and not rec[7]):
+                    need.append(rec)
+        need.sort(key=lambda rec: -rec[6])
+        for rec in need:
+            if clock[q].get(rec[2], 0) < rec[3]:
+                Q[q].wait_ge(T.sem[rec[2]], rec[3])
+                know(q, rec)
+
+    def note(q, reads, writes, sem, value, dma):
+        order[0] += 1
+        snap = dict(clock[q])
+        snap[sem] = max(value, snap.get(sem, 0))
+        for reg in writes:
+            log[reg[0]] = [rec for rec in log.get(reg[0], []) if not inside(reg, rec[0])]
+        for reg in reads:
+            log.setdefault(reg[0], []).append([reg, False, sem, value, q, snap, order[0], dma])
+        for reg in writes:
+            log.setdefault(reg[0], []).append([reg, True, sem, value, q, snap, order[0], dma])
+
+    def run(q, call, reads, writes):
+        settle(q, reads, writes, False)
+        sem = own[q]
+        count[sem] = count.get(sem, 0) + 1
+        call(Q[q]).then_inc(T.sem[sem], 1)
+        note(q, reads, writes, sem, count[sem], False)
+
+    def dma(q, call, reads, writes, sem, total):
+        settle(q, reads, writes, True)
+        count[sem] = count.get(sem, 0) + 16
+        call(Q[q]).then_inc(T.sem[sem], 16)
+        note(q, reads, writes, sem, 16 * total, True)
+
+    def remote(call, reads):
+        settle("g", reads, [], True)
+        call(Q["g"])
+
+    def landed(writes, sem, value):
+        order[0] += 1
+        for reg in writes:
+            log.setdefault(reg[0], []).append([reg, True, sem, value, "far", {sem: value}, order[0], True])
+
+    return {"run": run, "dma": dma, "remote": remote, "landed": landed, "count": count, "clock": clock, "Q": Q}
+
+
+def rank_program(g, core, T, topo):
+    rank = T.rank_of(core)
+    if rank is None:
+        return
+    F = flow(g, T)
+    run, dma = F["run"], F["dma"]
+    ADD, SUB, MUL = AluOpType.add, AluOpType.subtract, AluOpType.mult
+    Sign, Copy, Relu = ActivationFunctionType.Sign, ActivationFunctionType.Copy, ActivationFunctionType.Relu
+
+    def A(n, c0, c1, step=1, p0=0, p1=128):
+        return (T[n][p0:p1, c0:c1:step] if step > 1 else T[n][p0:p1, c0:c1], [(n, p0, p1, c0, c1, step, c0 % step)])
+
+    def K(n, c0, c1):
+        return (T[n][:, c0:c1].bitcast(dt.uint8), [(n, 0, 128, c0, c1, 1, 0)])
+
+    def K32(n, c0, c1):
+        return (T[n][:, c0:c1].bitcast(dt.uint32), [(n, 0, 128, c0, c1, 1, 0)])
+
+    def I(win, off):
+        return (win[0].indirect(off[0]), win[1] + off[1])
+
+    def P(bank, n):
+        return (T["ps"][:, 512 * bank:512 * bank + n], [("ps", 0, 128, 512 * bank, 512 * bank + 512, 1, 0)])
+
+    def sc(s):
+        return (s[0], s[1]) if isinstance(s, tuple) else (s, [])
+
+    def cp(out, in_, q="v"):
+        run(q, lambda e: e.tensor_copy(out[0], in_[0]), in_[1], out[1])
+
+    def tt(out, a, b, op):
+        run("v", lambda e: e.tensor_tensor(out[0], a[0], b[0], op), a[1] + b[1], out[1])
+
+    def ts(out, a, s1, op0, s2=None, op1=None):
+        x1, r1 = sc(s1)
+        x2, r2 = sc(s2)
+        if op1 is None:
+            run("v", lambda e: e.tensor_scalar(out[0], a[0], x1, None, op0), a[1] + r1, out[1])
+        else:
+            run("v", lambda e: e.tensor_scalar(out[0], a[0], x1, x2, op0, op1), a[1] + r1 + r2, out[1])
+
+    def tr(out, in_):
+        run("v", lambda e: e.transpose(out[0], in_[0]), in_[1], out[1])
+
+    def act(out, in_, f, scale=1.0, bias=0.0):
+        x, r = sc(scale)
+        run("s", lambda e: e.activation(out[0], in_[0], f, bias=bias, scale=x), in_[1] + r, out[1])
+
+    def quant(cq, cs, in_):
+        run("v", lambda e: e.quantize_mx(cq[0], cs[0], in_[0]), in_[1], cq[1] + cs[1])
+
+    def mm(out, wq, ws, xq, xs):
+        run("t", lambda e: e.matmul_mx(out[0], wq[0], ws[0], xq[0], xs[0], True, True), wq[1] + ws[1] + xq[1] + xs[1], out[1])
+
+    def load(q, out, in_, sem, total, reads=()):
+        dma(q, lambda e: e.dma_start(out[0], in_), list(reads), out[1], sem, total)
+
+    def iota(out, pattern, base, cm, loose=True):
+        if loose:
+            run("g", lambda e: e.iota(out[0], pattern, base, cm, allow_small_or_imprecise_dtypes=True), [], out[1])
+        else:
+            run("g", lambda e: e.iota(out[0], pattern, base, cm), [], out[1])
+
+    for k, (c0, c1) in enumerate(PIECES):
+        load("y", A("x0", 4 * c0, 4 * c1), T["x"][:, 4 * c0:4 * c1], "lx%d" % k, 1)
+    load("s", A("ut", 0, 512), T["u"][:, :], "lu", 1)
+    tabs = []
+    for a in range(4):
+        for h in range(2):
+            base = 32 * a + 16 * h
+            for t in range(7 - 2 * a):
+                tabs.append((base + t, base + t + 1, T["rho"][16 * (7 - t):16 * (8 - t), :]))
+            tabs.append((base + 7 - 2 * a, base + 8, T["lam"][0:16 * (2 * a + 1), :]))
+            if a == 0:
+                tabs.append((base + 9, base + 16, T["rho"][0:112, :]))
+            else:
+                tabs.append((base + 9, base + 15, T["rho"][32:128, :]))
+                tabs.append((base + 15, base + 16, T["lam"][112:128, :]))
+    for k, (p0, p1, src) in enumerate(tabs):
+        load("s" if k % 5 < 2 else "y", A("raw", 0, 896, 1, p0, p1), src, "ltab", len(tabs))
+    iota(A("pi", 0, 1), [[0, 1]], 0, 1, False)
+    iota(A("a2", 0, 8), [[2, 4], [0, 2]], 0, 0)
+    iota(A("ce", 0, 14), [[32, 14]], 0, 0)
+    iota(A("co", 0, 14), [[64, 7], [16, 2]], 0, 0)
+    iota(A("ident", 0, 896), [[1, 8], [0, 2], [8, 56]], 0, 0, False)
+    for k in range(8):
+        p = 16 * k + 8
+        dma("y", lambda e: e.dma_start(T["raw"][p:p + 1, :], T["ident"][p:p + 1, :]), A("ident", 0, 896)[1], A("raw", 0, 896, 1, p, p + 1)[1], "lid", 8)
+    load("y", K("wq", 0, 512), T["wc"][:, :], "lw", 2)
+    load("y", A("wsp", 0, 512), T["ws"][:, :], "lw", 2)
+    load("y", A("vt", 0, 512), T["v"][:, :], "lv", 1)
+    iota(A("cl", 0, 224), [[32, 14], [1, 16]], 0, 0)
+    iota(A("pr", 0, 896), [[0, 896]], 0, 0)
+    iota(A("pr2", 0, 896), [[0, 896]], 0, 0)
+    iota(A("ones", 0, 512), [[0, 512]], 1, 0)
+    for b in range(4):
+        o, i1 = A("et%d" % b, 0, 512), A("ones", 0, 512)
+        run("g", lambda e: e.affine_select(o[0], i1[0], [[1, 512]], AluOpType.is_equal, 0.0, -b, -4), i1[1], o[1])
+
+    def cc(k):
+        return A("cc", k, k + 1)
+
+    def gr(k):
+        return A("gr", 8 * k, 8 * k + 8)
+
+    def pc(k):
+        return A("pi2", k, k + 1)
+
+    ts(pc(0), A("pi", 0, 1), 15, AluOpType.bitwise_and)
+    ts(pc(1), A("pi", 0, 1), 31, AluOpType.bitwise_and)
+    ts(pc(2), A("pi", 0, 1), 5, AluOpType.arith_shift_right)
+    cp(cc(0), pc(0))
+    cp(cc(1), pc(1))
+    ts(cc(2), pc(2), 2.0, MUL)
+    ts(cc(3), cc(0), 2.0, MUL, -14.0, ADD)
+    ts(cc(5), cc(0), -1.0, MUL, 6.0, ADD)
+    ts(cc(7), cc(0), 8.0, AluOpType.is_lt)
+    ts(cc(8), cc(0), 15.0, AluOpType.is_equal, 7.0, MUL)
+    ts(gr(12), A("a2", 0, 8), cc(0), ADD, 6.0, AluOpType.not_equal)
+    ts(gr(0), A("a2", 0, 8), cc(0), ADD, 7.0, AluOpType.is_ge)
+    ts(gr(1), A("a2", 0, 8), cc(3), ADD)
+    ts(gr(3), gr(0), 2.0, MUL)
+    tt(gr(2), gr(0), gr(1), MUL)
+    ts(cc(9), cc(1), 2.0, MUL)
+    tt(gr(4), gr(2), gr(3), ADD)
+    tt(cc(10), cc(9), cc(0), SUB)
+    ts(gr(5), gr(4), cc(5), ADD)
+    ts(A("lef", 0, 14), A("ce", 0, 14), cc(1), ADD)
+    tt(gr(13), gr(5), gr(12), MUL)
+    ts(gr(6), gr(13), cc(7), MUL, cc(8), ADD)
+    ts(A("lof", 0, 14), A("co", 0, 14), cc(10), ADD)
+    ts(A("lb", 0, 8), gr(6), 16.0, MUL)
+    cp(A("le", 0, 14), A("lef", 0, 14))
+    cp(A("lo", 0, 14), A("lof", 0, 14))
+    ts(cc(12), cc(0), 7.0, AluOpType.is_lt, 448.0, MUL)
+    ts(cc(13), cc(0), 15.0, AluOpType.is_ge, 448.0, MUL)
+    ts(cc(11), cc(2), cc(0), ADD, 6.0, AluOpType.not_equal)
+    tt(cc(16), cc(12), cc(13), ADD)
+    ts(cc(14), cc(2), cc(0), ADD, 6.0, AluOpType.is_equal)
+    tt(cc(15), cc(1), cc(0), SUB)
+    SCB, GOES = cc(16), cc(11)
+    quant(A("uq", 0, 128), A("us", 0, 128), A("ut", 0, 512))
+    cp(K32("ubq", 0, 128), I(K32("uq", 0, 128), A("lb", 0, 8)))
+    cp(A("ubs", 0, 128), I(A("us", 0, 128), A("lb", 0, 8)))
+    SGN = cc(24)
+
+    def later_constants():
+        ts(cc(4), cc(0), -1.0, MUL, 7.0, ADD)
+        ts(cc(6), cc(0), 8.0, AluOpType.is_ge)
+        ts(gr(8), A("a2", 0, 8), 0.0, AluOpType.is_equal, 2.0, MUL)
+        ts(gr(7), gr(2), cc(4), ADD)
+        tt(gr(9), gr(8), A("a2", 0, 8), ADD)
+        ts(cc(18), cc(2), cc(0), ADD, 7.0, AluOpType.is_lt)
+        ts(cc(19), cc(2), 0.0, AluOpType.is_equal)
+        ts(cc(20), cc(0), 15.0, AluOpType.is_lt)
+        ts(gr(10), gr(9), cc(6), MUL)
+        tt(cc(21), cc(19), cc(20), AluOpType.max)
+        tt(gr(11), gr(7), gr(10), SUB)
+        tt(cc(23), cc(21), cc(6), MUL)
+        ts(gr(14), gr(11), 16.0, MUL, 1.0, ADD)
+        tt(cc(22), cc(18), cc(23), AluOpType.max)
+        ts(A("lf", 0, 8), gr(14), 113.0, AluOpType.min)
+        ts(SGN, cc(22), -2.0, MUL, 1.0, ADD)
+
+    def scores(r, k, bank, flips, bits):
+        c0, c1 = PIECES[k]
+        n = c1 - c0
+        xq, xs = A("xq%d" % r, c0, c1), A("xs%d" % r, c0, c1)
+        if flips:
+            mm(P(bank, n), A("ufq", 0, 128), A("ufs", 0, 128), xq, xs)
+            act(A("phi", c0, c1), P(bank, n), Sign, SGN, TINY)
+        if bits:
+            mm(P(bank + 1, n), A("ubq", 0, 128), A("ubs", 0, 128), xq, xs)
+            act(A("beta", c0, c1), P(bank + 1, n), Sign, 1.0, -TINY)
+
+    for k, (c0, c1) in enumerate(PIECES):
+        quant(A("xq0", c0, c1), A("xs0", c0, c1), A("x0", 4 * c0, 4 * c1))
+        scores(0, k, 2 * k, False, True)
+    later_constants()
+    for b in range(2):
+        for j in range(8):
+            ts(A("eo", 448 * b + j, 448 * b + 448, 8), A("raw", 112 * j + 56 * b, 112 * j + 56 * b + 56), GOES, MUL)
+    ts(A("labe", 0, 224), A("cl", 0, 224), cc(15), ADD, cc(14), MUL)
+
+    for r in range(3):
+        X = "x%d" % r
+        act(A("bo", 0, 224), I(A("beta", 0, 448), A("lo", 0, 14)), Relu, SCB)
+        act(A("be", 0, 224), I(A("beta", 0, 448), A("le", 0, 14)), Relu, SCB)
+        halves = [A("xh%d" % b, 0, C) for b in range(4)] + [A("xj", b * C, b * C + C) for b in range(4)]
+        for b in range(2):
+            act(halves[b], A(X, b, 4 * C, 4), Copy, 0.5)
+        tr(A("tbo", 0, 224), A("bo", 0, 224))
+        tt(A("be2", 0, 224), A("be", 0, 224), A("labe", 0, 224), ADD)
+        tt(A("ie", 0, 14), A("tbo", 15, 224, 16), A("lef", 0, 14), ADD)
+        cp(A("of0", 0, 14), A("ie", 0, 14))
+        for t in range(8):
+            bn, TT = "be2" if t % 2 == 0 else "bo", "t%d" % (t % 2)
+            for m0, m1 in HALVES:
+                tt(A("o%d" % (t % 2), 16 * m0, 16 * m1), I(A("eo", 0, 896), A("of%d" % t, m0, m1)), A(bn, 16 * m0, 16 * m1), ADD)
+            for m0, m1 in HALVES:
+                tr(A(TT, 16 * m0, 16 * m1), A("o%d" % (t % 2), 16 * m0, 16 * m1))
+            if t < 7:
+                for m0, m1 in HALVES:
+                    cp(A("of%d" % (t + 1), m0, m1), A(TT, 16 * m0 + t, 16 * m1, 16))
+            else:
+                for w, kap in ((0, 8), (1, 7)):
+                    for h in range(2):
+                        o, i1 = A("pr", 448 * w + 16 * h, 448 * w + 448, 32), A(TT, kap, 224, 16)
+                        if h:
+                            act(o, i1, Copy)
+                        else:
+                            cp(o, i1)
+            if t % 2 == 0:
+                a = (6 - t) // 2
+                p0, kap = 32 * a, 10 if a == 0 else 8 + 2 * a
+                act(A("mlf", 0, 28, 2, p0, p0 + 32), A(TT, kap, 224, 16, p0, p0 + 32), Copy)
+                act(A("mlf", 1, 28, 2, p0, p0 + 32), A(TT, 8, 224, 16, p0, p0 + 32), Copy, 1.0, 448.0)
+            if t < 6:
+                act(halves[2 + t], A(X, (2 + t) % 4, 4 * C, 4), Copy, 0.5)
+        cp(A("ml", 0, 28), A("mlf", 0, 28))
+        tr(A("rw", 0, 448), A("pr", 0, 448))
+        tr(A("rw", 448, 896), A("pr", 448, 896))
+        (c0, c1), (c2, c3) = PIECES
+        act(A("gk", c2, c3), I(A("rw", 0, 896), A("ml", c2 // 16, c3 // 16)), Copy)
+        cp(A("gk", c0, c1), I(A("rw", 0, 896), A("ml", c0 // 16, c1 // 16)))
+        tr(A("tk", c0, c1), A("gk", c0, c1))
+        tr(A("tk", c2, c3), A("gk", c2, c3))
+        for h in range(2):
+            for e in range(2):
+                cp(A("kn", 2 * h + e, 28, 4), A("tk", 32 * e + 16 * h, 448, 64))
+        dst = T.cores[rank ^ STEP[r]]
+        rid, pid = topo.addr(dst)[0], topo.addr(dst)[1]
+        eng = topo.mask(core, dst)
+        neng = len(topo.engines(core, dst))
+
+        def send(f, s, d, c0, c1, sem):
+            si, do = f(s, c0, c1), f(d, c0, c1)
+            F["remote"](lambda e: e.remote_dma(do[0], si[0], T.sem[sem], T.sem["sent"], pid, rid, eng), si[1])
+            F["count"]["sent"] = F["count"].get("sent", 0) + neng
+
+        KX, LK = "kx%d" % r, "lk%d" % r
+        cp(A("kp", 0, 14), A("kn", 0, 28, 2))
+        cp(A("kp", 14, 28), A("kn", 1, 28, 2))
+        cp(A(KX, 0, 28), A("kp", 0, 28))
+        for a in range(4):
+            lo, hi = 32 * a, 32 * a + 16
+            for p, q, i0 in ((lo, hi, 14), (hi, lo, 0)):
+                o, i1 = A(KX, 14 - i0, 28 - i0, 1, q, q + 16), A("kp", i0, i0 + 14, 1, p, p + 16)
+                dma("y", lambda e: e.dma_start(o[0], i1[0]), i1[1], o[1], "sw%d" % r, 8)
+        send(A, KX, LK, 0, 28, "ka%d" % r)
+        F["landed"](A(LK, 0, 28)[1], "ka%d" % r, neng)
+        for k, (c0, c1) in enumerate(PIECES):
+            kl = A("kn", c0 // 16, c1 // 16)
+            for b in range(4):
+                tt(A("vm", 4 * c0 + b, 4 * c1, 4), I(A("xh%d" % b, 0, C), kl), A("xj", b * C + c0, b * C + c1), ADD)
+            quant(A("vq", c0, c1), A("vs", c0, c1), A("vm", 4 * c0, 4 * c1))
+            for b in range(4):
+                mm(P(4 * k + b, c1 - c0), A("wq", 128 * b, 128 * b + 128), A("wsp", 128 * b, 128 * b + 128), A("vq", c0, c1), A("vs", c0, c1))
+            for b in range(4):
+                if k == 0 or b < 2:
+                    act(A("hl", 4 * c0 + b, 4 * c1, 4), P(4 * k + b, c1 - c0), Copy, 0.03125)
+        if r == 0:
+            for b in range(4):
+                quant(A("eq%d" % b, 0, 128), A("es%d" % b, 0, 128), A("et%d" % b, 0, 512))
+        for k, (c0, c1) in enumerate(PIECES):
+            if k == 1:
+                for b in (2, 3):
+                    ts(A("hl", 4 * c0 + b, 4 * c1, 4), P(4 * k + b, c1 - c0), 0.03125, MUL)
+            quant(A("hq%d" % r, c0, c1), A("hs%d" % r, c0, c1), A("hl", 4 * c0, 4 * c1))
+            send(K, "hq%d" % r, "lq%d" % r, c0, c1, "arr%d%d" % (r, k))
+            send(A, "hs%d" % r, "ls%d" % r, c0, c1, "arr%d%d" % (r, k))
+            F["landed"](A("lq%d" % r, c0, c1)[1] + A("ls%d" % r, c0, c1)[1], "arr%d%d" % (r, k), 2 * neng)
+        if r == 0:
+            tt(A("mt", 0, 448), A("eo", 0, 448), A("eo", 448, 896), ADD)
+            act(A("mm", 0, 448), A("mt", 0, 448), Copy, 0.5)
+            tt(A("dtb", 0, 448), A("eo", 448, 896), A("eo", 0, 448), SUB)
+            act(A("dd", 0, 448), A("dtb", 0, 448), Copy, 0.5)
+        cp(A("ml2", 0, 28, 2), A(KX, 0, 14))
+        ts(A("ml2", 1, 28, 2), A(KX, 14, 28), 448.0, ADD)
+        for w in range(2):
+            for h in range(2):
+                cp(A("pr2", 448 * w + 16 * h, 448 * w + 448, 32), A(LK, 14 * w, 14 * w + 14))
+            tr(A("rw2", 448 * w, 448 * w + 448), A("pr2", 448 * w, 448 * w + 448))
+        (c0, c1), (c2, c3) = PIECES
+        act(A("gk2", c2, c3), I(A("rw2", 0, 896), A("ml2", c2 // 16, c3 // 16)), Copy)
+        cp(A("gk2", c0, c1), I(A("rw2", 0, 896), A("ml2", c0 // 16, c1 // 16)))
+        tr(A("tk2", c0, c1), A("gk2", c0, c1))
+        tr(A("tk2", c2, c3), A("gk2", c2, c3))
+        cp(A("kk", 0, 28), A("tk2", 0, 448, 16))
+        if r == 0:
+            cp(K32("ufq", 0, 128), I(K32("uq", 0, 128), A("lf", 0, 8)))
+            cp(A("ufs", 0, 128), I(A("us", 0, 128), A("lf", 0, 8)))
+        if r == 1:
+            quant(A("vvq", 0, 128), A("vvs", 0, 128), A("vt", 0, 512))
+        for k, (c0, c1) in enumerate(PIECES):
+            for b in range(4):
+                mm(P(4 * k + b, c1 - c0), A("eq%d" % b, 0, 128), A("es%d" % b, 0, 128), A("lq%d" % r, c0, c1), A("ls%d" % r, c0, c1))
+            for b in range(4):
+                if b >= 2 and k == 1:
+                    cp(A("d%d" % b, c0, c1), P(4 * k + b, c1 - c0))
+                else:
+                    act(A("d%d" % b, c0, c1), P(4 * k + b, c1 - c0), Copy)
+        Y = "x%d" % (r + 1)
+        for k, (c0, c1) in enumerate(PIECES):
+            kl = A("kk", c0 // 16, c1 // 16)
+            for b in range(4):
+                tt(A(Y, 4 * c0 + b, 4 * c1, 4), I(A("d%d" % b, 0, C), kl), A("vm", 4 * c0 + b, 4 * c1, 4), ADD)
+            quant(A("xq%d" % (r + 1), c0, c1), A("xs%d" % (r + 1), c0, c1), A(Y, 4 * c0, 4 * c1))
+            scores(r + 1, k, 2 * k, True, r < 2)
+            if r == 2:
+                dma("y", lambda e: e.dma_start(T["oc"][:, 4 * c0:4 * c1], K("xq3", c0, c1)[0]), K("xq3", c0, c1)[1], [("oc", 0, 128, c0, c1, 1, 0)], "outs", 16)
+                for q in range(4):
+                    dma("y", lambda e: e.dma_start(T["osc"][4 * q:4 * q + 4, c0:c1], T["xs3"][32 * q:32 * q + 4, c0:c1]), A("xs3", c0, c1)[1], [("osc", 4 * q, 4 * q + 4, c0, c1, 1, 0)], "outs", 16)
+                mm(P(4 + k, c1 - c0), A("vvq", 0, 128), A("vvs", 0, 128), A("xq3", c0, c1), A("xs3", c0, c1))
+                act(A("yb", c0, c1), P(4 + k, c1 - c0), Copy)
+                dma("y", lambda e: e.dma_start(T["y"][:, c0:c1], T["yb"][:, c0:c1]), A("yb", c0, c1)[1], [("y", 0, 128, c0, c1, 1, 0)], "outs", 16)
+        for c0, c1 in PIECES:
+            tt(A("dd", c0, c1), A("dd", c0, c1), A("phi", c0, c1), MUL)
+            if r < 2:
+                tt(A("eo", c0, c1), A("mm", c0, c1), A("dd", c0, c1), SUB)
+                tt(A("eo", 448 + c0, 448 + c1), A("mm", c0, c1), A("dd", c0, c1), ADD)
+            else:
+                tt(A("lrb", 2 * c0, 2 * c1, 2), A("mm", c0, c1), A("dd", c0, c1), SUB)
+                tt(A("lrb", 2 * c0 + 1, 2 * c1, 2), A("mm", c0, c1), A("dd", c0, c1), ADD)
+    for g0, g1, half, p in ((0, 7, 1, 9), (7, 8, 1, 0), (0, 7, 0, 97), (7, 8, 0, 111)):
+        dma("y", lambda e: e.dma_start(T["lr"][g0:g1, 896 * half:896 * half + 896], T["lrb"][p:p + g1 - g0, :]), A("lrb", 0, 896, 1, p, p + g1 - g0)[1], [("lr", g0, g1, 896 * half, 896 * half + 896, 1, 0)], "outs", 16)
+    for sem in ("sv", "ss", "st", "sg", "sent", "outs"):
+        if F["clock"]["g"].get(sem, 0) < F["count"][sem]:
+            g.wait_ge(T.sem[sem], F["count"][sem])

@@ -3,66 +3,31 @@ from concourse.mybir import dt, AluOpType, ActivationFunctionType
 
 C = 448
 STEP = [1, 2, 3]
-PIECES = [(0, 256), (256, 448)]
-HALVES = [(0, 8), (8, 14)]
+VP = [(0, 160), (160, 320), (320, 448)]
+XP = [(0, 160), (160, 320), (320, 448)]
+CHAINS = [(0, 4), (4, 8)]
+SLOTS = (8, 6)
+MEET = 12
 TINY = 2.0 ** -100
+LB, LF, LE, LO, FL, ST, GO, FP, FM, FK, FE, FO = 0, 8, 16, 24, 32, 34, 36, 38, 42, 44, 46, 54
 
-SCRATCH = {
-    "ut": ("sbuf", [128, 512], "bfloat16"), "vt": ("sbuf", [128, 512], "bfloat16"),
-    "uq": ("sbuf", [128, 128], "float8_e4m3fn_x4"), "us": ("sbuf", [128, 128], "uint8"),
-    "vvq": ("sbuf", [128, 128], "float8_e4m3fn_x4"), "vvs": ("sbuf", [128, 128], "uint8"),
-    "ubq": ("sbuf", [128, 128], "float8_e4m3fn_x4"), "ubs": ("sbuf", [128, 128], "uint8"),
-    "ufq": ("sbuf", [128, 128], "float8_e4m3fn_x4"), "ufs": ("sbuf", [128, 128], "uint8"),
-    "wq": ("sbuf", [128, 512], "float8_e4m3fn_x4"), "wsp": ("sbuf", [128, 512], "uint8"),
-    "raw": ("sbuf", [128, 896], "int32"), "ident": ("sbuf", [128, 896], "int32"),
-    "pi": ("sbuf", [128, 1], "int32"), "pi2": ("sbuf", [128, 8], "int32"),
-    "a2": ("sbuf", [128, 8], "float32"), "cc": ("sbuf", [128, 32], "float32"),
-    "gr": ("sbuf", [128, 128], "float32"),
-    "ce": ("sbuf", [128, 14], "float32"), "co": ("sbuf", [128, 14], "float32"),
-    "lef": ("sbuf", [128, 14], "float32"), "lof": ("sbuf", [128, 14], "float32"),
-    "le": ("sbuf", [128, 14], "uint16"), "lo": ("sbuf", [128, 14], "uint16"),
-    "lb": ("sbuf", [128, 8], "uint16"), "lf": ("sbuf", [128, 8], "uint16"),
-    "ones": ("sbuf", [128, 512], "bfloat16"),
-    "eo": ("sbuf", [128, 896], "float32"), "mt": ("sbuf", [128, 448], "float32"), "dtb": ("sbuf", [128, 448], "float32"),
-    "mm": ("sbuf", [128, 448], "float32"), "dd": ("sbuf", [128, 448], "float32"), "lrb": ("sbuf", [128, 896], "float32"),
-    "phi": ("sbuf", [128, 448], "float32"), "beta": ("sbuf", [128, 448], "float32"),
-    "be": ("sbuf", [128, 224], "float32"), "bo": ("sbuf", [128, 224], "float32"),
-    "tbo": ("sbuf", [128, 224], "float32"),
-    "ie": ("sbuf", [128, 14], "float32"), "cl": ("sbuf", [128, 224], "float32"), "labe": ("sbuf", [128, 224], "float32"),
-    "be2": ("sbuf", [128, 224], "float32"), "mlf": ("sbuf", [128, 28], "float32"),
-    "kp": ("sbuf", [128, 28], "uint16"), "ml2": ("sbuf", [128, 28], "uint16"), "kk": ("sbuf", [128, 28], "uint16"),
-    "pr2": ("sbuf", [128, 896], "float32"), "rw2": ("sbuf", [128, 896], "float32"),
-    "gk2": ("sbuf", [128, 448], "float32"), "tk2": ("sbuf", [128, 448], "float32"),
-    "ml": ("sbuf", [128, 28], "uint16"), "kn": ("sbuf", [128, 28], "uint16"),
-    "pr": ("sbuf", [128, 896], "float32"), "rw": ("sbuf", [128, 896], "float32"),
-    "gk": ("sbuf", [128, 448], "float32"), "tk": ("sbuf", [128, 448], "float32"),
-    "xj": ("sbuf", [128, 4 * C], "bfloat16"), "vm": ("sbuf", [128, 4 * C], "bfloat16"), "vq": ("sbuf", [128, C], "float8_e4m3fn_x4"), "vs": ("sbuf", [128, C], "uint8"),
-    "hl": ("sbuf", [128, 4 * C], "bfloat16"), "yb": ("sbuf", [128, C], "float32"),
-    "ps": ("psum", [128, 4096], "float32"),
-}
-for _t in range(8):
-    SCRATCH["o%d" % (_t % 2)] = ("sbuf", [128, 224], "float32")
-    SCRATCH["t%d" % (_t % 2)] = ("sbuf", [128, 224], "float32")
-    SCRATCH["of%d" % _t] = ("sbuf", [128, 14], "uint16")
-for _b in range(4):
-    SCRATCH["xh%d" % _b] = ("sbuf", [128, C], "bfloat16")
-    SCRATCH["d%d" % _b] = ("sbuf", [128, C], "bfloat16")
-    SCRATCH["et%d" % _b] = ("sbuf", [128, 512], "bfloat16")
-    SCRATCH["eq%d" % _b] = ("sbuf", [128, 128], "float8_e4m3fn_x4")
-    SCRATCH["es%d" % _b] = ("sbuf", [128, 128], "uint8")
-for _r in range(4):
-    SCRATCH["x%d" % _r] = ("sbuf", [128, 4 * C], "bfloat16")
-    SCRATCH["xq%d" % _r] = ("sbuf", [128, C], "float8_e4m3fn_x4")
-    SCRATCH["xs%d" % _r] = ("sbuf", [128, C], "uint8")
-for _r in range(3):
-    SCRATCH["kx%d" % _r] = ("sbuf", [128, 28], "uint16")
-    SCRATCH["lk%d" % _r] = ("sbuf", [128, 28], "uint16")
-    SCRATCH["hq%d" % _r] = ("sbuf", [128, C], "float8_e4m3fn_x4")
-    SCRATCH["hs%d" % _r] = ("sbuf", [128, C], "uint8")
-    SCRATCH["lq%d" % _r] = ("sbuf", [128, C], "float8_e4m3fn_x4")
-    SCRATCH["ls%d" % _r] = ("sbuf", [128, C], "uint8")
+F32, U16, BF, X4, U8 = "float32", "uint16", "bfloat16", "float8_e4m3fn_x4", "uint8"
+SCRATCH = {"ps": ("psum", [128, 4096], F32)}
+for _names, _n, _d in (
+        ("ut vt ones et0 et1 et2 et3", 512, BF), ("uq vvq ubq ufq eq0 eq1 eq2 eq3", 128, X4), ("us vvs ubs ufs es0 es1 es2 es3", 128, U8),
+        ("wq", 512, X4), ("wsp", 512, U8), ("raw", 896, "int32"), ("img", 56, "int32"), ("pi", 16, "int32"), ("pb", 16, "int32"), ("pj", 16, "int32"),
+        ("pf", 16, F32), ("cc", 32, F32), ("sl", 16, F32), ("qa qb qc", 56, F32), ("ci cenc bo be oi ti", 128, F32), ("mli mlf", 28, F32),
+        ("fx", 64, U16), ("of", 56, U16), ("ml kn ml2 kk", 32, U16),
+        ("win d0 d1", 3 * C, F32), ("beta tk tk2 pr2", 512, F32), ("o", 256, F32), ("tt", 768, F32),
+        ("pr gk rw2 gk2 yb", C, F32), ("rw", 672, F32), ("kg", 16, F32), ("kx0 kx1 kx2 lk0 lk1 lk2", 32, F32),
+        ("ec oc2 sc dc mmc ddc dd3", 112, F32), ("lrb", 224, F32),
+        ("vm hl xj x0 x1 x2 x3", 4 * C, BF), ("xh0 xh1 xh2 xh3 da0 da1 da2 da3", C, BF),
+        ("vq xq0 xq1 xq2 xq3 hq0 hq1 hq2 lq0 lq1 lq2", C, X4), ("vs xs0 xs1 xs2 xs3 hs0 hs1 hs2 ls0 ls1 ls2", C, U8)):
+    for _name in _names.split():
+        SCRATCH[_name] = ("sbuf", [128, _n], _d)
 
-SEMAPHORES = ["sv", "ss", "st", "sg", "lx0", "lx1", "lu", "ltab", "lid", "lw", "lv", "sent", "outs"] + ["arr%d%d" % (r, k) for r in range(3) for k in range(2)] + ["ka%d" % r for r in range(3)] + ["sw%d" % r for r in range(3)]
+SEMAPHORES = (["sv", "ss", "st", "sg", "lu", "ltab", "lid", "lw", "lv", "sent", "outs"] + ["lx%d" % k for k in range(len(XP))]
+              + ["arr%d%d" % (r, k) for r in range(3) for k in range(len(VP))] + ["ka%d" % r for r in range(3)] + ["sw%d" % r for r in range(3)] + ["lh%d" % r for r in range(3)])
 
 
 def flow(g, T):
@@ -142,8 +107,8 @@ def rank_program(g, core, T, topo):
         return
     F = flow(g, T)
     run, dma = F["run"], F["dma"]
-    ADD, SUB, MUL = AluOpType.add, AluOpType.subtract, AluOpType.mult
-    Sign, Copy, Relu = ActivationFunctionType.Sign, ActivationFunctionType.Copy, ActivationFunctionType.Relu
+    ADD, SUB, MUL, AND = AluOpType.add, AluOpType.subtract, AluOpType.mult, AluOpType.bitwise_and
+    Sign, Copy = ActivationFunctionType.Sign, ActivationFunctionType.Copy
 
     def A(n, c0, c1, step=1, p0=0, p1=128):
         return (T[n][p0:p1, c0:c1:step] if step > 1 else T[n][p0:p1, c0:c1], [(n, p0, p1, c0, c1, step, c0 % step)])
@@ -160,11 +125,14 @@ def rank_program(g, core, T, topo):
     def P(bank, n):
         return (T["ps"][:, 512 * bank:512 * bank + n], [("ps", 0, 128, 512 * bank, 512 * bank + 512, 1, 0)])
 
+    def fx(c0, n):
+        return A("fx", c0, c0 + n)
+
     def sc(s):
         return (s[0], s[1]) if isinstance(s, tuple) else (s, [])
 
-    def cp(out, in_, q="v"):
-        run(q, lambda e: e.tensor_copy(out[0], in_[0]), in_[1], out[1])
+    def cp(out, in_):
+        run("v", lambda e: e.tensor_copy(out[0], in_[0]), in_[1], out[1])
 
     def tt(out, a, b, op):
         run("v", lambda e: e.tensor_tensor(out[0], a[0], b[0], op), a[1] + b[1], out[1])
@@ -177,195 +145,234 @@ def rank_program(g, core, T, topo):
         else:
             run("v", lambda e: e.tensor_scalar(out[0], a[0], x1, x2, op0, op1), a[1] + r1 + r2, out[1])
 
+    def state(out, in_):
+        ts(out, in_, -1.5, ADD, 1.0 / 6.0, MUL)
+
     def tr(out, in_):
         run("v", lambda e: e.transpose(out[0], in_[0]), in_[1], out[1])
 
-    def act(out, in_, f, scale=1.0, bias=0.0):
+    def fill(out, value):
+        run("v", lambda e: e.memset(out[0], value), [], out[1])
+
+    def act(out, in_, f=Copy, scale=1.0, bias=0.0):
         x, r = sc(scale)
         run("s", lambda e: e.activation(out[0], in_[0], f, bias=bias, scale=x), in_[1] + r, out[1])
 
-    def quant(cq, cs, in_):
+    def quant(q, s, c0, c1, tile):
+        cq, cs, in_ = A(q, c0, c1), A(s, c0, c1), A(tile, 4 * c0, 4 * c1)
         run("v", lambda e: e.quantize_mx(cq[0], cs[0], in_[0]), in_[1], cq[1] + cs[1])
 
-    def mm(out, wq, ws, xq, xs):
-        run("t", lambda e: e.matmul_mx(out[0], wq[0], ws[0], xq[0], xs[0], True, True), wq[1] + ws[1] + xq[1] + xs[1], out[1])
+    def mm(bank, wq, ws, w0, xq, xs, c0, c1):
+        out, ops = P(bank, c1 - c0), (A(wq, w0, w0 + 128), A(ws, w0, w0 + 128), A(xq, c0, c1), A(xs, c0, c1))
+        run("t", lambda e: e.matmul_mx(out[0], ops[0][0], ops[1][0], ops[2][0], ops[3][0], True, True), [x for o in ops for x in o[1]], out[1])
 
-    def load(q, out, in_, sem, total, reads=()):
-        dma(q, lambda e: e.dma_start(out[0], in_), list(reads), out[1], sem, total)
+    def load(q, out, in_, sem, total):
+        dma(q, lambda e: e.dma_start(out[0], in_), [], out[1], sem, total)
 
-    def iota(out, pattern, base, cm, loose=True):
-        if loose:
-            run("g", lambda e: e.iota(out[0], pattern, base, cm, allow_small_or_imprecise_dtypes=True), [], out[1])
-        else:
+    def move(q, out, in_, sem, total):
+        dma(q, lambda e: e.dma_start(out[0], in_[0]), in_[1], out[1], sem, total)
+
+    def iota(out, pattern, base=0, cm=0, whole=False):
+        if whole:
             run("g", lambda e: e.iota(out[0], pattern, base, cm), [], out[1])
+        else:
+            run("g", lambda e: e.iota(out[0], pattern, base, cm, allow_small_or_imprecise_dtypes=True), [], out[1])
 
-    for k, (c0, c1) in enumerate(PIECES):
-        load("y", A("x0", 4 * c0, 4 * c1), T["x"][:, 4 * c0:4 * c1], "lx%d" % k, 1)
     load("s", A("ut", 0, 512), T["u"][:, :], "lu", 1)
+    for k, (c0, c1) in enumerate(XP):
+        load("y", A("x0", 4 * c0, 4 * c1), T["x"][:, 4 * c0:4 * c1], "lx%d" % k, 1)
     tabs = []
-    for a in range(4):
-        for h in range(2):
-            base = 32 * a + 16 * h
-            for t in range(7 - 2 * a):
-                tabs.append((base + t, base + t + 1, T["rho"][16 * (7 - t):16 * (8 - t), :]))
-            tabs.append((base + 7 - 2 * a, base + 8, T["lam"][0:16 * (2 * a + 1), :]))
-            if a == 0:
-                tabs.append((base + 9, base + 16, T["rho"][0:112, :]))
-            else:
-                tabs.append((base + 9, base + 15, T["rho"][32:128, :]))
-                tabs.append((base + 15, base + 16, T["lam"][112:128, :]))
+    for q in range(4):
+        lo, hi = 16 * q, 64 + 16 * q
+        tabs += [(lo, lo + 8, T["lam"][:, :]), (lo + 8, lo + 16, T["lam"][:, :]), (hi + 8, hi + 16, T["rho"][:, :])]
+        tabs += [(hi + t, hi + t + 1, T["rho"][16 * (7 - t):16 * (8 - t), :]) for t in range(7)]
     for k, (p0, p1, src) in enumerate(tabs):
-        load("s" if k % 5 < 2 else "y", A("raw", 0, 896, 1, p0, p1), src, "ltab", len(tabs))
-    iota(A("pi", 0, 1), [[0, 1]], 0, 1, False)
-    iota(A("a2", 0, 8), [[2, 4], [0, 2]], 0, 0)
-    iota(A("ce", 0, 14), [[32, 14]], 0, 0)
-    iota(A("co", 0, 14), [[64, 7], [16, 2]], 0, 0)
-    iota(A("ident", 0, 896), [[1, 8], [0, 2], [8, 56]], 0, 0, False)
-    for k in range(8):
-        p = 16 * k + 8
-        dma("y", lambda e: e.dma_start(T["raw"][p:p + 1, :], T["ident"][p:p + 1, :]), A("ident", 0, 896)[1], A("raw", 0, 896, 1, p, p + 1)[1], "lid", 8)
+        load("s" if k % 2 else "y", A("raw", 0, 896, 1, p0, p1), src, "ltab", len(tabs))
+    iota(A("pi", 0, 1), [[0, 1]], 0, 1, True)
+    iota(A("qa", 0, 56), [[64, 7], [16, 2], [8, 4]])
+    iota(A("qb", 0, 56), [[0, 14], [16, 2], [0, 2]])
+    iota(A("pj", 0, 4), [[0, 4]], 16, 16, True)
+    iota(A("pj", 4, 8), [[0, 4]], 96 + 2048, -16, True)
+    iota(A("pj", 8, 12), [[0, 4]], 1, 16, True)
+    iota(A("sl", 0, 8), [[1, 8]])
+    iota(A("sl", 8, 16), [[64, 4], [16, 2]])
+    iota(A("ci", 0, 128), [[192, 8], [6, 16]], 3)
+    iota(A("mli", 0, 28), [[96, 14], [0, 2]], 6 * C + 3)
+
+    def bits(names, k0):
+        for k, mask in enumerate(names):
+            ts(A("pb", k0 + k, k0 + k + 1), A("pi", 0, 1), mask, AND)
+        cp(A("pf", k0, k0 + len(names)), A("pb", k0, k0 + len(names)))
+        return [A("pf", k0 + k, k0 + k + 1) for k in range(len(names))]
+
+    used = [0]
+
+    def col(a, s1, op0, s2=None, op1=None):
+        out = A("cc", used[0], used[0] + 1)
+        used[0] += 1
+        ts(out, a, s1, op0, s2, op1)
+        return out
+
+    def fixed(c0, n, step, base):
+        ts(fx(c0, n), A("sl", 0, n), float(step), MUL, base, ADD)
+
+    fill(A("win", 0, 3 * C, 3), 0.0)
+    p14, p31, p32, p16 = bits((14, 31, 32, 16), 0)
+    tt(A("qc", 0, 56), A("qa", 0, 56), A("qb", 0, 56), ADD)
+    ts(A("pj", 0, 12), A("pj", 0, 12), 113, AND)
+    ts(A("img", 0, 56), A("qc", 0, 56), col(p14, 0.5, MUL), ADD)
+    cp(fx(LB, 12), A("pj", 0, 12))
+    for q in range(4):
+        move("y", A("raw", 0, 896, 1, 71 + 16 * q, 72 + 16 * q), A("img", 0, 56, 1, 0, 16), "lid", 4)
     load("y", K("wq", 0, 512), T["wc"][:, :], "lw", 2)
     load("y", A("wsp", 0, 512), T["ws"][:, :], "lw", 2)
     load("y", A("vt", 0, 512), T["v"][:, :], "lv", 1)
-    iota(A("cl", 0, 224), [[32, 14], [1, 16]], 0, 0)
-    iota(A("pr", 0, 896), [[0, 896]], 0, 0)
-    iota(A("pr2", 0, 896), [[0, 896]], 0, 0)
-    iota(A("ones", 0, 512), [[0, 512]], 1, 0)
+    even = col(p32, 8.0, MUL, p31, ADD)
+    c48 = col(p32, 48.0, MUL)
+    p15, p1, p2, p12, p48, p64 = bits((15, 1, 2, 12, 48, 64), 4)
+    odd = col(even, p16, ADD)
+    cbase = col(p16, 6.0, MUL, c48, ADD)
+    fixed(LE, 8, 32, even)
+    far = col(p15, -7.5, ADD, 16.0, MUL)
+    ts(fx(LO, 8), A("sl", 8, 16), odd, ADD)
+    ts(A("cenc", 0, 128), A("ci", 0, 128), cbase, ADD, 6.0 * C - 3.0, AluOpType.min)
+    far = col(far, -1.0, MUL, far, AluOpType.max)
+    SGN = A("cc", 31, 32)
+    fill(A("cc", 31, 32, 1, 0, 64), 1.0)
+    far = col(far, -7.0, ADD)
+    fill(A("cc", 31, 32, 1, 64, 128), -1.0)
+    fixed(LF + 4, 4, 0, far)
+    fill(A("beta", C, 512), 1.0)
+    quant("uq", "us", 0, 128, "ut")
+    cp(K32("ubq", 0, 128), I(K32("uq", 0, 128), fx(LB, 8)))
+    run("s", lambda e: e.activation(T["ubs"][:, :], T["us"][:, :].indirect(fx(LB, 8)[0]), Copy), A("us", 0, 128)[1] + fx(LB, 8)[1], A("ubs", 0, 128)[1])
+    iota(A("pr", 0, C), [[0, C]])
+    iota(A("rw", C, 672), [[0, 672 - C]])
+    iota(A("tk", C, 512), [[0, 512 - C]])
+    iota(A("ones", 0, 512), [[0, 512]], 1)
     for b in range(4):
         o, i1 = A("et%d" % b, 0, 512), A("ones", 0, 512)
         run("g", lambda e: e.affine_select(o[0], i1[0], [[1, 512]], AluOpType.is_equal, 0.0, -b, -4), i1[1], o[1])
-
-    def cc(k):
-        return A("cc", k, k + 1)
-
-    def gr(k):
-        return A("gr", 8 * k, 8 * k + 8)
-
-    def pc(k):
-        return A("pi2", k, k + 1)
-
-    ts(pc(0), A("pi", 0, 1), 15, AluOpType.bitwise_and)
-    ts(pc(1), A("pi", 0, 1), 31, AluOpType.bitwise_and)
-    ts(pc(2), A("pi", 0, 1), 5, AluOpType.arith_shift_right)
-    cp(cc(0), pc(0))
-    cp(cc(1), pc(1))
-    ts(cc(2), pc(2), 2.0, MUL)
-    ts(cc(3), cc(0), 2.0, MUL, -14.0, ADD)
-    ts(cc(5), cc(0), -1.0, MUL, 6.0, ADD)
-    ts(cc(7), cc(0), 8.0, AluOpType.is_lt)
-    ts(cc(8), cc(0), 15.0, AluOpType.is_equal, 7.0, MUL)
-    ts(gr(12), A("a2", 0, 8), cc(0), ADD, 6.0, AluOpType.not_equal)
-    ts(gr(0), A("a2", 0, 8), cc(0), ADD, 7.0, AluOpType.is_ge)
-    ts(gr(1), A("a2", 0, 8), cc(3), ADD)
-    ts(gr(3), gr(0), 2.0, MUL)
-    tt(gr(2), gr(0), gr(1), MUL)
-    ts(cc(9), cc(1), 2.0, MUL)
-    tt(gr(4), gr(2), gr(3), ADD)
-    tt(cc(10), cc(9), cc(0), SUB)
-    ts(gr(5), gr(4), cc(5), ADD)
-    ts(A("lef", 0, 14), A("ce", 0, 14), cc(1), ADD)
-    tt(gr(13), gr(5), gr(12), MUL)
-    ts(gr(6), gr(13), cc(7), MUL, cc(8), ADD)
-    ts(A("lof", 0, 14), A("co", 0, 14), cc(10), ADD)
-    ts(A("lb", 0, 8), gr(6), 16.0, MUL)
-    cp(A("le", 0, 14), A("lef", 0, 14))
-    cp(A("lo", 0, 14), A("lof", 0, 14))
-    ts(cc(12), cc(0), 7.0, AluOpType.is_lt, 448.0, MUL)
-    ts(cc(13), cc(0), 15.0, AluOpType.is_ge, 448.0, MUL)
-    ts(cc(11), cc(2), cc(0), ADD, 6.0, AluOpType.not_equal)
-    tt(cc(16), cc(12), cc(13), ADD)
-    ts(cc(14), cc(2), cc(0), ADD, 6.0, AluOpType.is_equal)
-    tt(cc(15), cc(1), cc(0), SUB)
-    SCB, GOES = cc(16), cc(11)
-    quant(A("uq", 0, 128), A("us", 0, 128), A("ut", 0, 512))
-    cp(K32("ubq", 0, 128), I(K32("uq", 0, 128), A("lb", 0, 8)))
-    cp(A("ubs", 0, 128), I(A("us", 0, 128), A("lb", 0, 8)))
-    SGN = cc(24)
+    iota(A("tk2", C, 512), [[0, 512 - C]])
+    iota(A("pr2", 0, C), [[0, C]])
+    iota(A("d0", 0, 3 * C, 3), [[0, C]])
+    iota(A("d0", 2, 3 * C, 3), [[0, C]], -1)
 
     def later_constants():
-        ts(cc(4), cc(0), -1.0, MUL, 7.0, ADD)
-        ts(cc(6), cc(0), 8.0, AluOpType.is_ge)
-        ts(gr(8), A("a2", 0, 8), 0.0, AluOpType.is_equal, 2.0, MUL)
-        ts(gr(7), gr(2), cc(4), ADD)
-        tt(gr(9), gr(8), A("a2", 0, 8), ADD)
-        ts(cc(18), cc(2), cc(0), ADD, 7.0, AluOpType.is_lt)
-        ts(cc(19), cc(2), 0.0, AluOpType.is_equal)
-        ts(cc(20), cc(0), 15.0, AluOpType.is_lt)
-        ts(gr(10), gr(9), cc(6), MUL)
-        tt(cc(21), cc(19), cc(20), AluOpType.max)
-        tt(gr(11), gr(7), gr(10), SUB)
-        tt(cc(23), cc(21), cc(6), MUL)
-        ts(gr(14), gr(11), 16.0, MUL, 1.0, ADD)
-        tt(cc(22), cc(18), cc(23), AluOpType.max)
-        ts(A("lf", 0, 8), gr(14), 113.0, AluOpType.min)
-        ts(SGN, cc(22), -2.0, MUL, 1.0, ADD)
+        same = col(p16, 4.0, MUL, p64, AluOpType.is_equal)
+        a = col(p1, 32.0, MUL)
+        other = col(p1, 16.0, MUL, p16, AluOpType.not_equal)
+        row = col(same, 6.0, MUL)
+        a = col(p12, 16.0, MUL, a, ADD)
+        other = col(other, 16.0, MUL)
+        b = col(p15, 32.0, MUL, row, ADD)
+        a = col(p2, 8.0, MUL, a, ADD)
+        c = col(p12, 0.25, MUL, other, ADD)
+        b = col(p1, -16.0, MUL, b, ADD)
+        a = col(a, row, ADD)
+        d = col(p14, 0.5, MUL, other, ADD)
+        ts(fx(ST, 1), p16, 2.0, MUL, b, ADD)
+        fixed(FL, 2, 256, a)
+        e = col(p15, 16.0, MUL)
+        b = col(b, 32.0, ADD)
+        f = col(p48, 21.0, MUL, 1.0, ADD)
+        e = col(p16, 0.5, MUL, e, ADD)
+        ts(fx(GO, 1), p16, -2.0, MUL, b, ADD)
+        f = col(p15, 3.0, MUL, f, ADD)
+        fixed(FP, 4, 4, c)
+        fixed(FM, 2, 8, d)
+        fixed(FK, 2, 256, e)
+        fixed(FE, 7, 48, f)
+        h = col(p15, 6.0, MUL)
+        ts(fx(FO, 7), fx(FE, 7), 1.0, ADD)
+        ts(A("mlf", 0, 28), A("mli", 0, 28), h, ADD)
 
-    def scores(r, k, bank, flips, bits):
-        c0, c1 = PIECES[k]
-        n = c1 - c0
-        xq, xs = A("xq%d" % r, c0, c1), A("xs%d" % r, c0, c1)
-        if flips:
-            mm(P(bank, n), A("ufq", 0, 128), A("ufs", 0, 128), xq, xs)
-            act(A("phi", c0, c1), P(bank, n), Sign, SGN, TINY)
-        if bits:
-            mm(P(bank + 1, n), A("ubq", 0, 128), A("ubs", 0, 128), xq, xs)
-            act(A("beta", c0, c1), P(bank + 1, n), Sign, 1.0, -TINY)
+    def scores(r, k):
+        c0, c1 = XP[k]
+        xq, xs = "xq%d" % r, "xs%d" % r
+        if r < 3:
+            mm(2 * k, "ubq", "ubs", 0, xq, xs, c0, c1)
+            act(A("beta", c0, c1), P(2 * k, c1 - c0), Sign, 1.0, -TINY)
+        if r > 0:
+            mm(2 * k + 1, "ufq", "ufs", 0, xq, xs, c0, c1)
+            act(A("d0", 3 * c0 + 1, 3 * c1, 3), P(2 * k + 1, c1 - c0), Sign, SGN, TINY)
 
-    for k, (c0, c1) in enumerate(PIECES):
-        quant(A("xq0", c0, c1), A("xs0", c0, c1), A("x0", 4 * c0, 4 * c1))
-        scores(0, k, 2 * k, False, True)
+    def halves(r, k):
+        c0, c1 = XP[k]
+        return [(A("xh%d" % b, c0, c1), A("x%d" % r, 4 * c0 + b, 4 * c1, 4)) for b in range(4)]
+
+    def recolour(k):
+        o, a, b = [A(n, 3 * XP[k][0], 3 * XP[k][1]) for n in ("win", "d0", "d1")]
+        run("v", lambda e: e.tensor_tensor_scan(o[0], a[0], b[0], 0.0, MUL, ADD), a[1] + b[1], o[1])
+
+    last = len(XP) - 1
+    for k, (c0, c1) in enumerate(XP):
+        quant("xq0", "xs0", c0, c1, "x0")
+        scores(0, k)
+        if k < last:
+            for o, i1 in halves(0, k):
+                act(o, i1, Copy, 0.5)
+    cp(K32("ufq", 0, 128), I(K32("uq", 0, 128), fx(LF, 8)))
     later_constants()
-    for b in range(2):
-        for j in range(8):
-            ts(A("eo", 448 * b + j, 448 * b + 448, 8), A("raw", 112 * j + 56 * b, 112 * j + 56 * b + 56), GOES, MUL)
-    ts(A("labe", 0, 224), A("cl", 0, 224), cc(15), ADD, cc(14), MUL)
 
+    def lay_tables(b):
+        for j in range(8):
+            ts(A("win", 3 * j + 1 + b, 3 * C, 24), A("raw", 112 * j + 56 * b, 112 * j + 56 * b + 56), 6.0, MUL, 3.0, ADD)
+
+    BETA, WIN = A("beta", 0, 512), A("win", 0, 3 * C)
     for r in range(3):
-        X = "x%d" % r
-        act(A("bo", 0, 224), I(A("beta", 0, 448), A("lo", 0, 14)), Relu, SCB)
-        act(A("be", 0, 224), I(A("beta", 0, 448), A("le", 0, 14)), Relu, SCB)
-        halves = [A("xh%d" % b, 0, C) for b in range(4)] + [A("xj", b * C, b * C + C) for b in range(4)]
-        for b in range(2):
-            act(halves[b], A(X, b, 4 * C, 4), Copy, 0.5)
-        tr(A("tbo", 0, 224), A("bo", 0, 224))
-        tt(A("be2", 0, 224), A("be", 0, 224), A("labe", 0, 224), ADD)
-        tt(A("ie", 0, 14), A("tbo", 15, 224, 16), A("lef", 0, 14), ADD)
-        cp(A("of0", 0, 14), A("ie", 0, 14))
-        for t in range(8):
-            bn, TT = "be2" if t % 2 == 0 else "bo", "t%d" % (t % 2)
-            for m0, m1 in HALVES:
-                tt(A("o%d" % (t % 2), 16 * m0, 16 * m1), I(A("eo", 0, 896), A("of%d" % t, m0, m1)), A(bn, 16 * m0, 16 * m1), ADD)
-            for m0, m1 in HALVES:
-                tr(A(TT, 16 * m0, 16 * m1), A("o%d" % (t % 2), 16 * m0, 16 * m1))
-            if t < 7:
-                for m0, m1 in HALVES:
-                    cp(A("of%d" % (t + 1), m0, m1), A(TT, 16 * m0 + t, 16 * m1, 16))
-            else:
-                for w, kap in ((0, 8), (1, 7)):
-                    for h in range(2):
-                        o, i1 = A("pr", 448 * w + 16 * h, 448 * w + 448, 32), A(TT, kap, 224, 16)
-                        if h:
-                            act(o, i1, Copy)
-                        else:
-                            cp(o, i1)
-            if t % 2 == 0:
-                a = (6 - t) // 2
-                p0, kap = 32 * a, 10 if a == 0 else 8 + 2 * a
-                act(A("mlf", 0, 28, 2, p0, p0 + 32), A(TT, kap, 224, 16, p0, p0 + 32), Copy)
-                act(A("mlf", 1, 28, 2, p0, p0 + 32), A(TT, 8, 224, 16, p0, p0 + 32), Copy, 1.0, 448.0)
-            if t < 6:
-                act(halves[2 + t], A(X, (2 + t) % 4, 4 * C, 4), Copy, 0.5)
-        cp(A("ml", 0, 28), A("mlf", 0, 28))
-        tr(A("rw", 0, 448), A("pr", 0, 448))
-        tr(A("rw", 448, 896), A("pr", 448, 896))
-        (c0, c1), (c2, c3) = PIECES
-        act(A("gk", c2, c3), I(A("rw", 0, 896), A("ml", c2 // 16, c3 // 16)), Copy)
-        cp(A("gk", c0, c1), I(A("rw", 0, 896), A("ml", c0 // 16, c1 // 16)))
-        tr(A("tk", c0, c1), A("gk", c0, c1))
-        tr(A("tk", c2, c3), A("gk", c2, c3))
-        for h in range(2):
-            for e in range(2):
-                cp(A("kn", 2 * h + e, 28, 4), A("tk", 32 * e + 16 * h, 448, 64))
+        fillers = [lambda: lay_tables(0), lambda: lay_tables(1), lambda: None] if r == 0 else [lambda k=k: recolour(k) for k in range(len(XP))]
+        fillers[0]()
+        tt(A("oi", 0, 128), I(BETA, fx(LE, 8)), A("cenc", 0, 128), ADD)
+        act(A("bo", 0, 128), I(BETA, fx(LO, 8)))
+        act(A("be", 0, 128), I(BETA, fx(LE, 8)))
+        fillers[1]()
+        tr(A("ti", 0, 128), A("oi", 0, 128))
+        for f in fillers[2:]:
+            f()
+        ts(A("of", 0, 8), A("ti", 7, 128, 16), 0.5, MUL)
+        rest = halves(r, last)
+        for t in range(7):
+            bn, o0, t0 = "bo" if t % 2 == 0 else "be", 128 * (t % 2), 128 * t
+            for m0, m1 in CHAINS:
+                tt(A("o", o0 + 16 * m0, o0 + 16 * m1), I(WIN, A("of", 8 * t + m0, 8 * t + m1)), A(bn, 16 * m0, 16 * m1), ADD)
+            if t == 6:
+                break
+            for m0, m1 in CHAINS:
+                tr(A("tt", t0 + 16 * m0, t0 + 16 * m1), A("o", o0 + 16 * m0, o0 + 16 * m1))
+            for m0, m1 in CHAINS:
+                ts(A("of", 8 * t + 8 + m0, 8 * t + 8 + m1), A("tt", t0 + 16 * m0 + t, t0 + 16 * m1, 16), 0.5, MUL)
+            gl = t + 1
+            row = 6 if gl % 2 == gl // 4 else 0
+            for a, n in enumerate(SLOTS):
+                act(A("pr", 256 * a + row, 256 * a + 32 * n, 16, 32 * (gl // 2), 32 * (gl // 2) + 32), A("tt", t0 + t, t0 + 16 * n, 8, 32 * a, 32 * a + 32))
+            if t % 2 == 1:
+                for c, gr in ((t, 6 - t), (7, 7 - t)):
+                    for a, n in enumerate(SLOTS):
+                        act(A("mlf", 16 * a + gr % 2, 16 * a + 2 * n, 2, 32 * (gr // 2), 32 * (gr // 2) + 32), A("tt", t0 + c, t0 + 16 * n, 16, 64 + 32 * a, 96 + 32 * a))
+            elif t < 4:
+                for b in (t, t + 1):
+                    act(rest[b][0], rest[b][1], Copy, 0.5)
+                    move("y", A("xj", b * C, b * C + C), A("xh%d" % b, 0, C), "lh%d" % r, 4)
+        tr(A("rw", 0, C), A("pr", 0, C))
+        for a, n in enumerate(SLOTS):
+            act(A("rw", C + 128 * a, C + 128 * a + 16 * n, 1, 96, 128), A("o", 0, 16 * n, 1, 32 * a, 32 * a + 32))
+            act(A("rw", C + 128 * a, C + 128 * a + 16 * n, 1, 0, 32), A("o", 0, 16 * n, 1, 64 + 32 * a, 96 + 32 * a))
+        state(A("ml", 0, 28), A("mlf", 0, 28))
+
+        def meeting(win, lst, got, out):
+            act(A(got, 16 * MEET, C), I(win, A(lst, MEET, 28)))
+            cp(A(got, 0, 16 * MEET), I(win, A(lst, 0, MEET)))
+            tr(A(out, 0, 16 * MEET), A(got, 0, 16 * MEET))
+            tr(A(out, 16 * MEET, C), A(got, 16 * MEET, C))
+
+        meeting(A("rw", 0, 672), "ml", "gk", "tk")
+        TK, KX, LK = A("tk", 0, 512), "kx%d" % r, "lk%d" % r
+        state(A("kn", 0, 32), I(TK, fx(FL, 2)))
+        act(A("kg", 0, 16), I(TK, fx(GO, 1)))
+        act(A(KX, 0, 16), I(TK, fx(ST, 1)))
+        for p in range(0, 128, 16):
+            move("y", A(KX, 16, 32, 1, p ^ 16, (p ^ 16) + 16), A("kg", 0, 16, 1, p, p + 16), "sw%d" % r, 8)
         dst = T.cores[rank ^ STEP[r]]
         rid, pid = topo.addr(dst)[0], topo.addr(dst)[1]
         eng = topo.mask(core, dst)
@@ -376,92 +383,88 @@ def rank_program(g, core, T, topo):
             F["remote"](lambda e: e.remote_dma(do[0], si[0], T.sem[sem], T.sem["sent"], pid, rid, eng), si[1])
             F["count"]["sent"] = F["count"].get("sent", 0) + neng
 
-        KX, LK = "kx%d" % r, "lk%d" % r
-        cp(A("kp", 0, 14), A("kn", 0, 28, 2))
-        cp(A("kp", 14, 28), A("kn", 1, 28, 2))
-        cp(A(KX, 0, 28), A("kp", 0, 28))
-        for a in range(4):
-            lo, hi = 32 * a, 32 * a + 16
-            for p, q, i0 in ((lo, hi, 14), (hi, lo, 0)):
-                o, i1 = A(KX, 14 - i0, 28 - i0, 1, q, q + 16), A("kp", i0, i0 + 14, 1, p, p + 16)
-                dma("y", lambda e: e.dma_start(o[0], i1[0]), i1[1], o[1], "sw%d" % r, 8)
-        send(A, KX, LK, 0, 28, "ka%d" % r)
-        F["landed"](A(LK, 0, 28)[1], "ka%d" % r, neng)
-        for k, (c0, c1) in enumerate(PIECES):
-            kl = A("kn", c0 // 16, c1 // 16)
+        send(A, KX, LK, 0, 32, "ka%d" % r)
+        F["landed"](A(LK, 0, 32)[1], "ka%d" % r, neng)
+        hq, hs, lq, ls = "hq%d" % r, "hs%d" % r, "lq%d" % r, "ls%d" % r
+
+        def ship(k):
+            c0, c1 = VP[k]
+            quant(hq, hs, c0, c1, "hl")
+            send(K, hq, lq, c0, c1, "arr%d%d" % (r, k))
+            send(A, hs, ls, c0, c1, "arr%d%d" % (r, k))
+            F["landed"](A(lq, c0, c1)[1] + A(ls, c0, c1)[1], "arr%d%d" % (r, k), 2 * neng)
+
+        for k, (c0, c1) in enumerate(VP):
             for b in range(4):
-                tt(A("vm", 4 * c0 + b, 4 * c1, 4), I(A("xh%d" % b, 0, C), kl), A("xj", b * C + c0, b * C + c1), ADD)
-            quant(A("vq", c0, c1), A("vs", c0, c1), A("vm", 4 * c0, 4 * c1))
+                tt(A("vm", 4 * c0 + b, 4 * c1, 4), I(A("xh%d" % b, 0, C), A("kn", c0 // 16, c1 // 16)), A("xj", b * C + c0, b * C + c1), ADD)
+            quant("vq", "vs", c0, c1, "vm")
             for b in range(4):
-                mm(P(4 * k + b, c1 - c0), A("wq", 128 * b, 128 * b + 128), A("wsp", 128 * b, 128 * b + 128), A("vq", c0, c1), A("vs", c0, c1))
+                mm(4 * (k % 2) + b, "wq", "wsp", 128 * b, "vq", "vs", c0, c1)
+            if k > 0:
+                ship(k - 1)
             for b in range(4):
-                if k == 0 or b < 2:
-                    act(A("hl", 4 * c0 + b, 4 * c1, 4), P(4 * k + b, c1 - c0), Copy, 0.03125)
-        if r == 0:
-            for b in range(4):
-                quant(A("eq%d" % b, 0, 128), A("es%d" % b, 0, 128), A("et%d" % b, 0, 512))
-        for k, (c0, c1) in enumerate(PIECES):
-            if k == 1:
-                for b in (2, 3):
-                    ts(A("hl", 4 * c0 + b, 4 * c1, 4), P(4 * k + b, c1 - c0), 0.03125, MUL)
-            quant(A("hq%d" % r, c0, c1), A("hs%d" % r, c0, c1), A("hl", 4 * c0, 4 * c1))
-            send(K, "hq%d" % r, "lq%d" % r, c0, c1, "arr%d%d" % (r, k))
-            send(A, "hs%d" % r, "ls%d" % r, c0, c1, "arr%d%d" % (r, k))
-            F["landed"](A("lq%d" % r, c0, c1)[1] + A("ls%d" % r, c0, c1)[1], "arr%d%d" % (r, k), 2 * neng)
-        if r == 0:
-            tt(A("mt", 0, 448), A("eo", 0, 448), A("eo", 448, 896), ADD)
-            act(A("mm", 0, 448), A("mt", 0, 448), Copy, 0.5)
-            tt(A("dtb", 0, 448), A("eo", 448, 896), A("eo", 0, 448), SUB)
-            act(A("dd", 0, 448), A("dtb", 0, 448), Copy, 0.5)
-        cp(A("ml2", 0, 28, 2), A(KX, 0, 14))
-        ts(A("ml2", 1, 28, 2), A(KX, 14, 28), 448.0, ADD)
-        for w in range(2):
-            for h in range(2):
-                cp(A("pr2", 448 * w + 16 * h, 448 * w + 448, 32), A(LK, 14 * w, 14 * w + 14))
-            tr(A("rw2", 448 * w, 448 * w + 448), A("pr2", 448 * w, 448 * w + 448))
-        (c0, c1), (c2, c3) = PIECES
-        act(A("gk2", c2, c3), I(A("rw2", 0, 896), A("ml2", c2 // 16, c3 // 16)), Copy)
-        cp(A("gk2", c0, c1), I(A("rw2", 0, 896), A("ml2", c0 // 16, c1 // 16)))
-        tr(A("tk2", c0, c1), A("gk2", c0, c1))
-        tr(A("tk2", c2, c3), A("gk2", c2, c3))
-        cp(A("kk", 0, 28), A("tk2", 0, 448, 16))
-        if r == 0:
-            cp(K32("ufq", 0, 128), I(K32("uq", 0, 128), A("lf", 0, 8)))
-            cp(A("ufs", 0, 128), I(A("us", 0, 128), A("lf", 0, 8)))
-        if r == 1:
-            quant(A("vvq", 0, 128), A("vvs", 0, 128), A("vt", 0, 512))
-        for k, (c0, c1) in enumerate(PIECES):
-            for b in range(4):
-                mm(P(4 * k + b, c1 - c0), A("eq%d" % b, 0, 128), A("es%d" % b, 0, 128), A("lq%d" % r, c0, c1), A("ls%d" % r, c0, c1))
-            for b in range(4):
-                if b >= 2 and k == 1:
-                    cp(A("d%d" % b, c0, c1), P(4 * k + b, c1 - c0))
+                o, i1 = A("hl", 4 * c0 + b, 4 * c1, 4), P(4 * (k % 2) + b, c1 - c0)
+                if k == len(VP) - 1 and b % 2 == 1:
+                    ts(o, i1, 0.03125, MUL)
                 else:
-                    act(A("d%d" % b, c0, c1), P(4 * k + b, c1 - c0), Copy)
-        Y = "x%d" % (r + 1)
-        for k, (c0, c1) in enumerate(PIECES):
-            kl = A("kk", c0 // 16, c1 // 16)
+                    act(o, i1, Copy, 0.03125)
+        ship(len(VP) - 1)
+        if r == 0:
+            run("s", lambda e: e.activation(T["ufs"][:, :], T["us"][:, :].indirect(fx(LF, 8)[0]), Copy), A("us", 0, 128)[1] + fx(LF, 8)[1], A("ufs", 0, 128)[1])
             for b in range(4):
-                tt(A(Y, 4 * c0 + b, 4 * c1, 4), I(A("d%d" % b, 0, C), kl), A("vm", 4 * c0 + b, 4 * c1, 4), ADD)
-            quant(A("xq%d" % (r + 1), c0, c1), A("xs%d" % (r + 1), c0, c1), A(Y, 4 * c0, 4 * c1))
-            scores(r + 1, k, 2 * k, True, r < 2)
+                quant("eq%d" % b, "es%d" % b, 0, 128, "et%d" % b)
+        act(A("pr2", 0, 512, 8), I(A(LK, 0, 32), fx(FP, 4)))
+        state(A("ml2", 0, 32), I(A(KX, 0, 32), fx(FM, 2)))
+        if r == 0:
+            tt(A("d1", 2, 3 * C, 3), A("win", 1, 3 * C, 3), A("win", 2, 3 * C, 3), ADD)
+            act(A("d1", 1, 3 * C, 3), A("d1", 2, 3 * C, 3), Copy, 0.5)
+        if r == 2:
+            act(A("ec", 0, 112), I(WIN, fx(FE, 7)), Copy, 1.0 / 6.0)
+            act(A("oc2", 0, 112), I(WIN, fx(FO, 7)), Copy, 1.0 / 6.0)
+        tr(A("rw2", 0, C), A("pr2", 0, C))
+        meeting(A("rw2", 0, C), "ml2", "gk2", "tk2")
+        state(A("kk", 0, 32), I(A("tk2", 0, 512), fx(FK, 2)))
+        if r == 0:
+            tt(A("d1", 0, 3 * C, 3), A("win", 1, 3 * C, 3), A("d1", 1, 3 * C, 3), SUB)
+        if r == 1:
+            tt(A("d1", 0, 3 * C, 3), A("d1", 0, 3 * C, 3), A("d0", 1, 3 * C, 3), MUL)
+        if r == 2:
+            tt(A("sc", 0, 112), A("ec", 0, 112), A("oc2", 0, 112), ADD)
+            tt(A("dc", 0, 112), A("ec", 0, 112), A("oc2", 0, 112), SUB)
+            act(A("mmc", 0, 112), A("sc", 0, 112), Copy, 0.5, -0.5)
+            act(A("ddc", 0, 112), A("dc", 0, 112), Copy, 0.5)
+            quant("vvq", "vvs", 0, 128, "vt")
+        for k, (c0, c1) in enumerate(VP):
+            for b in range(4):
+                mm(4 * ((k + 1) % 2) + b, "eq%d" % b, "es%d" % b, 0, lq, ls, c0, c1)
+            for b in range(4):
+                o, i1 = A("da%d" % b, c0, c1), P(4 * ((k + 1) % 2) + b, c1 - c0)
+                if k == len(VP) - 1 and b % 2 == 1:
+                    cp(o, i1)
+                else:
+                    act(o, i1)
+        Y, yq, ys = "x%d" % (r + 1), "xq%d" % (r + 1), "xs%d" % (r + 1)
+        outs = 8 + 6 * len(XP)
+        for k, (c0, c1) in enumerate(XP):
+            for b in range(4):
+                tt(A(Y, 4 * c0 + b, 4 * c1, 4), I(A("da%d" % b, 0, C), A("kk", c0 // 16, c1 // 16)), A("vm", 4 * c0 + b, 4 * c1, 4), ADD)
+            quant(yq, ys, c0, c1, Y)
+            scores(r + 1, k)
+            if r < 2 and k < last:
+                for o, i1 in halves(r + 1, k):
+                    act(o, i1, Copy, 0.5)
             if r == 2:
-                dma("y", lambda e: e.dma_start(T["oc"][:, 4 * c0:4 * c1], K("xq3", c0, c1)[0]), K("xq3", c0, c1)[1], [("oc", 0, 128, c0, c1, 1, 0)], "outs", 16)
+                mm(2 * k, "vvq", "vvs", 0, yq, ys, c0, c1)
+                act(A("yb", c0, c1), P(2 * k, c1 - c0))
+                move("y", (T["oc"][:, 4 * c0:4 * c1], [("oc", 0, 128, c0, c1, 1, 0)]), K(yq, c0, c1), "outs", outs)
                 for q in range(4):
-                    dma("y", lambda e: e.dma_start(T["osc"][4 * q:4 * q + 4, c0:c1], T["xs3"][32 * q:32 * q + 4, c0:c1]), A("xs3", c0, c1)[1], [("osc", 4 * q, 4 * q + 4, c0, c1, 1, 0)], "outs", 16)
-                mm(P(4 + k, c1 - c0), A("vvq", 0, 128), A("vvs", 0, 128), A("xq3", c0, c1), A("xs3", c0, c1))
-                act(A("yb", c0, c1), P(4 + k, c1 - c0), Copy)
-                dma("y", lambda e: e.dma_start(T["y"][:, c0:c1], T["yb"][:, c0:c1]), A("yb", c0, c1)[1], [("y", 0, 128, c0, c1, 1, 0)], "outs", 16)
-        for c0, c1 in PIECES:
-            tt(A("dd", c0, c1), A("dd", c0, c1), A("phi", c0, c1), MUL)
-            if r < 2:
-                tt(A("eo", c0, c1), A("mm", c0, c1), A("dd", c0, c1), SUB)
-                tt(A("eo", 448 + c0, 448 + c1), A("mm", c0, c1), A("dd", c0, c1), ADD)
-            else:
-                tt(A("lrb", 2 * c0, 2 * c1, 2), A("mm", c0, c1), A("dd", c0, c1), SUB)
-                tt(A("lrb", 2 * c0 + 1, 2 * c1, 2), A("mm", c0, c1), A("dd", c0, c1), ADD)
-    for g0, g1, half, p in ((0, 7, 1, 9), (7, 8, 1, 0), (0, 7, 0, 97), (7, 8, 0, 111)):
-        dma("y", lambda e: e.dma_start(T["lr"][g0:g1, 896 * half:896 * half + 896], T["lrb"][p:p + g1 - g0, :]), A("lrb", 0, 896, 1, p, p + g1 - g0)[1], [("lr", g0, g1, 896 * half, 896 * half + 896, 1, 0)], "outs", 16)
+                    move("y", (T["osc"][4 * q:4 * q + 4, c0:c1], [("osc", 4 * q, 4 * q + 4, c0, c1, 1, 0)]), A(ys, c0, c1, 1, 32 * q, 32 * q + 4), "outs", outs)
+                move("y", (T["y"][:, c0:c1], [("y", 0, 128, c0, c1, 1, 0)]), A("yb", c0, c1), "outs", outs)
+    tt(A("dd3", 0, 112), I(A("d0", 0, 3 * C), fx(FE, 7)), A("ddc", 0, 112), MUL)
+    tt(A("lrb", 0, 224, 2), A("mmc", 0, 112), A("dd3", 0, 112), ADD)
+    tt(A("lrb", 1, 224, 2), A("mmc", 0, 112), A("dd3", 0, 112), SUB)
+    for q in range(8):
+        move("s" if q % 2 else "y", (T["lr"][:, 224 * q:224 * q + 224], [("lr", 0, 8, 224 * q, 224 * q + 224, 1, 0)]), A("lrb", 0, 224, 1, 16 * q + 8, 16 * q + 16), "outs", outs)
     for sem in ("sv", "ss", "st", "sg", "sent", "outs"):
         if F["clock"]["g"].get(sem, 0) < F["count"][sem]:
             g.wait_ge(T.sem[sem], F["count"][sem])

import numpy as np
from concourse.mybir import dt, AluOpType, ActivationFunctionType

C = 448
STEP = [1, 2, 3]
VP = [(0, 160), (160, 320), (320, 448)]
XP = [(0, 160), (160, 320), (320, 448)]
CHAINS = [(0, 4), (4, 8)]
SLOTS = (8, 6)
MEET = 12
TINY = 2.0 ** -100
LB, LF, LE, LO, FL, ST, GO, FP, FM, FK, FE, FO = 0, 8, 16, 24, 32, 34, 36, 38, 42, 44, 46, 54

F32, U16, BF, X4, U8 = "float32", "uint16", "bfloat16", "float8_e4m3fn_x4", "uint8"
SCRATCH = {"ps": ("psum", [128, 4096], F32)}
for _names, _n, _d in (
        ("ut vt ones et0 et1 et2 et3", 512, BF), ("uq vvq ubq ufq eq0 eq1 eq2 eq3", 128, X4), ("us vvs ubs ufs es0 es1 es2 es3", 128, U8),
        ("wq", 512, X4), ("wsp", 512, U8), ("raw", 896, "int32"), ("img", 56, "int32"), ("pi", 16, "int32"), ("pb", 16, "int32"), ("pj", 16, "int32"),
        ("pf", 16, F32), ("cc", 32, F32), ("sl", 16, F32), ("qa qb qc", 56, F32), ("ci cenc bo be oi ti", 128, F32), ("mli mlf", 28, F32),
        ("fx", 64, U16), ("of", 56, U16), ("ml kn ml2 kk", 32, U16),
        ("win d0 d1", 3 * C, F32), ("beta tk tk2 pr2", 512, F32), ("o", 256, F32), ("tt", 768, F32),
        ("pr gk rw2 gk2 yb", C, F32), ("rw", 672, F32), ("kg", 16, F32), ("kx0 kx1 kx2 lk0 lk1 lk2", 32, F32),
        ("ec oc2 sc dc mmc ddc dd3", 112, F32), ("lrb", 224, F32),
        ("vm hl xj x0 x1 x2 x3", 4 * C, BF), ("xh0 xh1 xh2 xh3 da0 da1 da2 da3", C, BF),
        ("vq xq0 xq1 xq2 xq3 hq0 hq1 hq2 lq0 lq1 lq2", C, X4), ("vs xs0 xs1 xs2 xs3 hs0 hs1 hs2 ls0 ls1 ls2", C, U8)):
    for _name in _names.split():
        SCRATCH[_name] = ("sbuf", [128, _n], _d)

SEMAPHORES = (["sv", "ss", "st", "sg", "lu", "ltab", "lid", "lw", "lv", "sent", "outs"] + ["lx%d" % k for k in range(len(XP))]
              + ["arr%d%d" % (r, k) for r in range(3) for k in range(len(VP))] + ["ka%d" % r for r in range(3)] + ["sw%d" % r for r in range(3)] + ["lh%d" % r for r in range(3)])


def flow(g, T):
    Q = {"v": g.vector, "s": g.scalar, "t": g.tensor, "g": g, "y": g.sync}
    own = {"v": "sv", "s": "ss", "t": "st", "g": "sg"}
    count = {}
    clock = {q: {} for q in Q}
    log = {}
    order = [0]

    def meet(a, b):
        return a[1] < b[2] and b[1] < a[2] and a[3] < b[4] and b[3] < a[4] and not (a[5] == b[5] and a[6] != b[6])

    def inside(a, b):
        return a[1] <= b[1] and b[2] <= a[2] and a[3] <= b[3] and b[4] <= a[4] and (a[5] == 1 or (a[5] == b[5] and a[6] == b[6]))

    def know(q, rec):
        for s, n in rec[5].items():
            if clock[q].get(s, 0) < n:
                clock[q][s] = n

    def settle(q, reads, writes, dma):
        need = []
        for reg in reads:
            for rec in log.get(reg[0], []):
                if rec[1] and meet(reg, rec[0]):
                    need.append(rec)
        for reg in writes:
            for rec in log.get(reg[0], []):
                if meet(reg, rec[0]) and not (not rec[1] and rec[4] == q and not dma and not rec[7]):
                    need.append(rec)
        need.sort(key=lambda rec: -rec[6])
        for rec in need:
            if clock[q].get(rec[2], 0) < rec[3]:
                Q[q].wait_ge(T.sem[rec[2]], rec[3])
                know(q, rec)

    def note(q, reads, writes, sem, value, dma):
        order[0] += 1
        snap = dict(clock[q])
        snap[sem] = max(value, snap.get(sem, 0))
        for reg in writes:
            log[reg[0]] = [rec for rec in log.get(reg[0], []) if not inside(reg, rec[0])]
        for reg in reads:
            log.setdefault(reg[0], []).append([reg, False, sem, value, q, snap, order[0], dma])
        for reg in writes:
            log.setdefault(reg[0], []).append([reg, True, sem, value, q, snap, order[0], dma])

    def run(q, call, reads, writes):
        settle(q, reads, writes, False)
        sem = own[q]
        count[sem] = count.get(sem, 0) + 1
        call(Q[q]).then_inc(T.sem[sem], 1)
        note(q, reads, writes, sem, count[sem], False)

    def dma(q, call, reads, writes, sem, total):
        settle(q, reads, writes, True)
        count[sem] = count.get(sem, 0) + 16
        call(Q[q]).then_inc(T.sem[sem], 16)
        note(q, reads, writes, sem, 16 * total, True)

    def remote(call, reads):
        settle("g", reads, [], True)
        call(Q["g"])

    def landed(writes, sem, value):
        order[0] += 1
        for reg in writes:
            log.setdefault(reg[0], []).append([reg, True, sem, value, "far", {sem: value}, order[0], True])

    return {"run": run, "dma": dma, "remote": remote, "landed": landed, "count": count, "clock": clock, "Q": Q}


def rank_program(g, core, T, topo):
    rank = T.rank_of(core)
    if rank is None:
        return
    F = flow(g, T)
    run, dma = F["run"], F["dma"]
    ADD, SUB, MUL, AND = AluOpType.add, AluOpType.subtract, AluOpType.mult, AluOpType.bitwise_and
    Sign, Copy = ActivationFunctionType.Sign, ActivationFunctionType.Copy

    def A(n, c0, c1, step=1, p0=0, p1=128):
        return (T[n][p0:p1, c0:c1:step] if step > 1 else T[n][p0:p1, c0:c1], [(n, p0, p1, c0, c1, step, c0 % step)])

    def K(n, c0, c1):
        return (T[n][:, c0:c1].bitcast(dt.uint8), [(n, 0, 128, c0, c1, 1, 0)])

    def K32(n, c0, c1):
        return (T[n][:, c0:c1].bitcast(dt.uint32), [(n, 0, 128, c0, c1, 1, 0)])

    def I(win, off):
        return (win[0].indirect(off[0]), win[1] + off[1])

    def P(bank, n):
        return (T["ps"][:, 512 * bank:512 * bank + n], [("ps", 0, 128, 512 * bank, 512 * bank + 512, 1, 0)])

    def fx(c0, n):
        return A("fx", c0, c0 + n)

    def sc(s):
        return (s[0], s[1]) if isinstance(s, tuple) else (s, [])

    def cp(out, in_):
        run("v", lambda e: e.tensor_copy(out[0], in_[0]), in_[1], out[1])

    def tt(out, a, b, op):
        run("v", lambda e: e.tensor_tensor(out[0], a[0], b[0], op), a[1] + b[1], out[1])

    def ts(out, a, s1, op0, s2=None, op1=None):
        x1, r1 = sc(s1)
        x2, r2 = sc(s2)
        if op1 is None:
            run("v", lambda e: e.tensor_scalar(out[0], a[0], x1, None, op0), a[1] + r1, out[1])
        else:
            run("v", lambda e: e.tensor_scalar(out[0], a[0], x1, x2, op0, op1), a[1] + r1 + r2, out[1])

    def state(out, in_):
        ts(out, in_, -1.5, ADD, 1.0 / 6.0, MUL)

    def tr(out, in_):
        run("v", lambda e: e.transpose(out[0], in_[0]), in_[1], out[1])

    def fill(out, value):
        run("v", lambda e: e.memset(out[0], value), [], out[1])

    def act(out, in_, f=Copy, scale=1.0, bias=0.0):
        x, r = sc(scale)
        run("s", lambda e: e.activation(out[0], in_[0], f, bias=bias, scale=x), in_[1] + r, out[1])

    def quant(q, s, c0, c1, tile):
        cq, cs, in_ = A(q, c0, c1), A(s, c0, c1), A(tile, 4 * c0, 4 * c1)
        run("v", lambda e: e.quantize_mx(cq[0], cs[0], in_[0]), in_[1], cq[1] + cs[1])

    def mm(bank, wq, ws, w0, xq, xs, c0, c1):
        out, ops = P(bank, c1 - c0), (A(wq, w0, w0 + 128), A(ws, w0, w0 + 128), A(xq, c0, c1), A(xs, c0, c1))
        run("t", lambda e: e.matmul_mx(out[0], ops[0][0], ops[1][0], ops[2][0], ops[3][0], True, True), [x for o in ops for x in o[1]], out[1])

    def load(q, out, in_, sem, total):
        dma(q, lambda e: e.dma_start(out[0], in_), [], out[1], sem, total)

    def move(q, out, in_, sem, total):
        dma(q, lambda e: e.dma_start(out[0], in_[0]), in_[1], out[1], sem, total)

    def iota(out, pattern, base=0, cm=0, whole=False):
        if whole:
            run("g", lambda e: e.iota(out[0], pattern, base, cm), [], out[1])
        else:
            run("g", lambda e: e.iota(out[0], pattern, base, cm, allow_small_or_imprecise_dtypes=True), [], out[1])

    load("s", A("ut", 0, 512), T["u"][:, :], "lu", 1)
    for k, (c0, c1) in enumerate(XP):
        load("y", A("x0", 4 * c0, 4 * c1), T["x"][:, 4 * c0:4 * c1], "lx%d" % k, 1)
    tabs = []
    for q in range(4):
        lo, hi = 16 * q, 64 + 16 * q
        tabs += [(lo, lo + 8, T["lam"][:, :]), (lo + 8, lo + 16, T["lam"][:, :]), (hi + 8, hi + 16, T["rho"][:, :])]
        tabs += [(hi + t, hi + t + 1, T["rho"][16 * (7 - t):16 * (8 - t), :]) for t in range(7)]
    for k, (p0, p1, src) in enumerate(tabs):
        load("s" if k % 2 else "y", A("raw", 0, 896, 1, p0, p1), src, "ltab", len(tabs))
    iota(A("pi", 0, 1), [[0, 1]], 0, 1, True)
    iota(A("qa", 0, 56), [[64, 7], [16, 2], [8, 4]])
    iota(A("qb", 0, 56), [[0, 14], [16, 2], [0, 2]])
    iota(A("pj", 0, 4), [[0, 4]], 16, 16, True)
    iota(A("pj", 4, 8), [[0, 4]], 96 + 2048, -16, True)
    iota(A("pj", 8, 12), [[0, 4]], 1, 16, True)
    iota(A("sl", 0, 8), [[1, 8]])
    iota(A("sl", 8, 16), [[64, 4], [16, 2]])
    iota(A("ci", 0, 128), [[192, 8], [6, 16]], 3)
    iota(A("mli", 0, 28), [[96, 14], [0, 2]], 6 * C + 3)

    def bits(names, k0):
        for k, mask in enumerate(names):
            ts(A("pb", k0 + k, k0 + k + 1), A("pi", 0, 1), mask, AND)
        cp(A("pf", k0, k0 + len(names)), A("pb", k0, k0 + len(names)))
        return [A("pf", k0 + k, k0 + k + 1) for k in range(len(names))]

    used = [0]

    def col(a, s1, op0, s2=None, op1=None):
        out = A("cc", used[0], used[0] + 1)
        used[0] += 1
        ts(out, a, s1, op0, s2, op1)
        return out

    def fixed(c0, n, step, base):
        ts(fx(c0, n), A("sl", 0, n), float(step), MUL, base, ADD)

    fill(A("win", 0, 3 * C, 3), 0.0)
    p14, p31, p32, p16 = bits((14, 31, 32, 16), 0)
    tt(A("qc", 0, 56), A("qa", 0, 56), A("qb", 0, 56), ADD)
    ts(A("pj", 0, 12), A("pj", 0, 12), 113, AND)
    ts(A("img", 0, 56), A("qc", 0, 56), col(p14, 0.5, MUL), ADD)
    cp(fx(LB, 12), A("pj", 0, 12))
    for q in range(4):
        move("y", A("raw", 0, 896, 1, 71 + 16 * q, 72 + 16 * q), A("img", 0, 56, 1, 0, 16), "lid", 4)
    load("y", K("wq", 0, 512), T["wc"][:, :], "lw", 2)
    load("y", A("wsp", 0, 512), T["ws"][:, :], "lw", 2)
    load("y", A("vt", 0, 512), T["v"][:, :], "lv", 1)
    even = col(p32, 8.0, MUL, p31, ADD)
    c48 = col(p32, 48.0, MUL)
    p15, p1, p2, p12, p48, p64 = bits((15, 1, 2, 12, 48, 64), 4)
    odd = col(even, p16, ADD)
    cbase = col(p16, 6.0, MUL, c48, ADD)
    fixed(LE, 8, 32, even)
    far = col(p15, -7.5, ADD, 16.0, MUL)
    ts(fx(LO, 8), A("sl", 8, 16), odd, ADD)
    ts(A("cenc", 0, 128), A("ci", 0, 128), cbase, ADD, 6.0 * C - 3.0, AluOpType.min)
    far = col(far, -1.0, MUL, far, AluOpType.max)
    SGN = A("cc", 31, 32)
    fill(A("cc", 31, 32, 1, 0, 64), 1.0)
    far = col(far, -7.0, ADD)
    fill(A("cc", 31, 32, 1, 64, 128), -1.0)
    fixed(LF + 4, 4, 0, far)
    fill(A("beta", C, 512), 1.0)
    quant("uq", "us", 0, 128, "ut")
    cp(K32("ubq", 0, 128), I(K32("uq", 0, 128), fx(LB, 8)))
    run("s", lambda e: e.activation(T["ubs"][:, :], T["us"][:, :].indirect(fx(LB, 8)[0]), Copy), A("us", 0, 128)[1] + fx(LB, 8)[1], A("ubs", 0, 128)[1])
    iota(A("pr", 0, C), [[0, C]])
    iota(A("rw", C, 672), [[0, 672 - C]])
    iota(A("tk", C, 512), [[0, 512 - C]])
    iota(A("ones", 0, 512), [[0, 512]], 1)
    for b in range(4):
        o, i1 = A("et%d" % b, 0, 512), A("ones", 0, 512)
        run("g", lambda e: e.affine_select(o[0], i1[0], [[1, 512]], AluOpType.is_equal, 0.0, -b, -4), i1[1], o[1])
    iota(A("tk2", C, 512), [[0, 512 - C]])
    iota(A("pr2", 0, C), [[0, C]])
    iota(A("d0", 0, 3 * C, 3), [[0, C]])
    iota(A("d0", 2, 3 * C, 3), [[0, C]], -1)

    def later_constants():
        same = col(p16, 4.0, MUL, p64, AluOpType.is_equal)
        a = col(p1, 32.0, MUL)
        other = col(p1, 16.0, MUL, p16, AluOpType.not_equal)
        row = col(same, 6.0, MUL)
        a = col(p12, 16.0, MUL, a, ADD)
        other = col(other, 16.0, MUL)
        b = col(p15, 32.0, MUL, row, ADD)
        a = col(p2, 8.0, MUL, a, ADD)
        c = col(p12, 0.25, MUL, other, ADD)
        b = col(p1, -16.0, MUL, b, ADD)
        a = col(a, row, ADD)
        d = col(p14, 0.5, MUL, other, ADD)
        ts(fx(ST, 1), p16, 2.0, MUL, b, ADD)
        fixed(FL, 2, 256, a)
        e = col(p15, 16.0, MUL)
        b = col(b, 32.0, ADD)
        f = col(p48, 21.0, MUL, 1.0, ADD)
        e = col(p16, 0.5, MUL, e, ADD)
        ts(fx(GO, 1), p16, -2.0, MUL, b, ADD)
        f = col(p15, 3.0, MUL, f, ADD)
        fixed(FP, 4, 4, c)
        fixed(FM, 2, 8, d)
        fixed(FK, 2, 256, e)
        fixed(FE, 7, 48, f)
        h = col(p15, 6.0, MUL)
        ts(fx(FO, 7), fx(FE, 7), 1.0, ADD)
        ts(A("mlf", 0, 28), A("mli", 0, 28), h, ADD)

    def scores(r, k):
        c0, c1 = XP[k]
        xq, xs = "xq%d" % r, "xs%d" % r
        if r < 3:
            mm(2 * k, "ubq", "ubs", 0, xq, xs, c0, c1)
            act(A("beta", c0, c1), P(2 * k, c1 - c0), Sign, 1.0, -TINY)
        if r > 0:
            mm(2 * k + 1, "ufq", "ufs", 0, xq, xs, c0, c1)
            act(A("d0", 3 * c0 + 1, 3 * c1, 3), P(2 * k + 1, c1 - c0), Sign, SGN, TINY)

    def halves(r, k):
        c0, c1 = XP[k]
        return [(A("xh%d" % b, c0, c1), A("x%d" % r, 4 * c0 + b, 4 * c1, 4)) for b in range(4)]

    def recolour(k):
        o, a, b = [A(n, 3 * XP[k][0], 3 * XP[k][1]) for n in ("win", "d0", "d1")]
        run("v", lambda e: e.tensor_tensor_scan(o[0], a[0], b[0], 0.0, MUL, ADD), a[1] + b[1], o[1])

    last = len(XP) - 1
    for k, (c0, c1) in enumerate(XP):
        quant("xq0", "xs0", c0, c1, "x0")
        scores(0, k)
        if k < last:
            for o, i1 in halves(0, k):
                act(o, i1, Copy, 0.5)
    cp(K32("ufq", 0, 128), I(K32("uq", 0, 128), fx(LF, 8)))
    later_constants()

    def lay_tables(b):
        for j in range(8):
            ts(A("win", 3 * j + 1 + b, 3 * C, 24), A("raw", 112 * j + 56 * b, 112 * j + 56 * b + 56), 6.0, MUL, 3.0, ADD)

    BETA, WIN = A("beta", 0, 512), A("win", 0, 3 * C)
    for r in range(3):
        fillers = [lambda: lay_tables(0), lambda: lay_tables(1), lambda: None] if r == 0 else [lambda k=k: recolour(k) for k in range(len(XP))]
        fillers[0]()
        tt(A("oi", 0, 128), I(BETA, fx(LE, 8)), A("cenc", 0, 128), ADD)
        act(A("bo", 0, 128), I(BETA, fx(LO, 8)))
        act(A("be", 0, 128), I(BETA, fx(LE, 8)))
        fillers[1]()
        tr(A("ti", 0, 128), A("oi", 0, 128))
        for f in fillers[2:]:
            f()
        ts(A("of", 0, 8), A("ti", 7, 128, 16), 0.5, MUL)
        rest = halves(r, last)
        for t in range(7):
            bn, o0, t0 = "bo" if t % 2 == 0 else "be", 128 * (t % 2), 128 * t
            for m0, m1 in CHAINS:
                tt(A("o", o0 + 16 * m0, o0 + 16 * m1), I(WIN, A("of", 8 * t + m0, 8 * t + m1)), A(bn, 16 * m0, 16 * m1), ADD)
            if t == 6:
                break
            for m0, m1 in CHAINS:
                tr(A("tt", t0 + 16 * m0, t0 + 16 * m1), A("o", o0 + 16 * m0, o0 + 16 * m1))
            for m0, m1 in CHAINS:
                ts(A("of", 8 * t + 8 + m0, 8 * t + 8 + m1), A("tt", t0 + 16 * m0 + t, t0 + 16 * m1, 16), 0.5, MUL)
            gl = t + 1
            row = 6 if gl % 2 == gl // 4 else 0
            for a, n in enumerate(SLOTS):
                act(A("pr", 256 * a + row, 256 * a + 32 * n, 16, 32 * (gl // 2), 32 * (gl // 2) + 32), A("tt", t0 + t, t0 + 16 * n, 8, 32 * a, 32 * a + 32))
            if t % 2 == 1:
                for c, gr in ((t, 6 - t), (7, 7 - t)):
                    for a, n in enumerate(SLOTS):
                        act(A("mlf", 16 * a + gr % 2, 16 * a + 2 * n, 2, 32 * (gr // 2), 32 * (gr // 2) + 32), A("tt", t0 + c, t0 + 16 * n, 16, 64 + 32 * a, 96 + 32 * a))
            elif t < 4:
                for b in (t, t + 1):
                    act(rest[b][0], rest[b][1], Copy, 0.5)
                    move("y", A("xj", b * C, b * C + C), A("xh%d" % b, 0, C), "lh%d" % r, 4)
        tr(A("rw", 0, C), A("pr", 0, C))
        for a, n in enumerate(SLOTS):
            act(A("rw", C + 128 * a, C + 128 * a + 16 * n, 1, 96, 128), A("o", 0, 16 * n, 1, 32 * a, 32 * a + 32))
            act(A("rw", C + 128 * a, C + 128 * a + 16 * n, 1, 0, 32), A("o", 0, 16 * n, 1, 64 + 32 * a, 96 + 32 * a))
        state(A("ml", 0, 28), A("mlf", 0, 28))

        def meeting(win, lst, got, out):
            act(A(got, 16 * MEET, C), I(win, A(lst, MEET, 28)))
            cp(A(got, 0, 16 * MEET), I(win, A(lst, 0, MEET)))
            tr(A(out, 0, 16 * MEET), A(got, 0, 16 * MEET))
            tr(A(out, 16 * MEET, C), A(got, 16 * MEET, C))

        meeting(A("rw", 0, 672), "ml", "gk", "tk")
        TK, KX, LK = A("tk", 0, 512), "kx%d" % r, "lk%d" % r
        state(A("kn", 0, 32), I(TK, fx(FL, 2)))
        act(A("kg", 0, 16), I(TK, fx(GO, 1)))
        act(A(KX, 0, 16), I(TK, fx(ST, 1)))
        for p in range(0, 128, 16):
            move("y", A(KX, 16, 32, 1, p ^ 16, (p ^ 16) + 16), A("kg", 0, 16, 1, p, p + 16), "sw%d" % r, 8)
        dst = T.cores[rank ^ STEP[r]]
        rid, pid = topo.addr(dst)[0], topo.addr(dst)[1]
        eng = topo.mask(core, dst)
        neng = len(topo.engines(core, dst))

        def send(f, s, d, c0, c1, sem):
            si, do = f(s, c0, c1), f(d, c0, c1)
            F["remote"](lambda e: e.remote_dma(do[0], si[0], T.sem[sem], T.sem["sent"], pid, rid, eng), si[1])
            F["count"]["sent"] = F["count"].get("sent", 0) + neng

        send(A, KX, LK, 0, 32, "ka%d" % r)
        F["landed"](A(LK, 0, 32)[1], "ka%d" % r, neng)
        hq, hs, lq, ls = "hq%d" % r, "hs%d" % r, "lq%d" % r, "ls%d" % r

        def ship(k):
            c0, c1 = VP[k]
            quant(hq, hs, c0, c1, "hl")
            send(K, hq, lq, c0, c1, "arr%d%d" % (r, k))
            send(A, hs, ls, c0, c1, "arr%d%d" % (r, k))
            F["landed"](A(lq, c0, c1)[1] + A(ls, c0, c1)[1], "arr%d%d" % (r, k), 2 * neng)

        for k, (c0, c1) in enumerate(VP):
            for b in range(4):
                tt(A("vm", 4 * c0 + b, 4 * c1, 4), I(A("xh%d" % b, 0, C), A("kn", c0 // 16, c1 // 16)), A("xj", b * C + c0, b * C + c1), ADD)
            quant("vq", "vs", c0, c1, "vm")
            for b in range(4):
                mm(4 * (k % 2) + b, "wq", "wsp", 128 * b, "vq", "vs", c0, c1)
            if k > 0:
                ship(k - 1)
            for b in range(4):
                o, i1 = A("hl", 4 * c0 + b, 4 * c1, 4), P(4 * (k % 2) + b, c1 - c0)
                if k == len(VP) - 1 and b % 2 == 1:
                    ts(o, i1, 0.03125, MUL)
                else:
                    act(o, i1, Copy, 0.03125)
        ship(len(VP) - 1)
        if r == 0:
            run("s", lambda e: e.activation(T["ufs"][:, :], T["us"][:, :].indirect(fx(LF, 8)[0]), Copy), A("us", 0, 128)[1] + fx(LF, 8)[1], A("ufs", 0, 128)[1])
            for b in range(4):
                quant("eq%d" % b, "es%d" % b, 0, 128, "et%d" % b)
        act(A("pr2", 0, 512, 8), I(A(LK, 0, 32), fx(FP, 4)))
        state(A("ml2", 0, 32), I(A(KX, 0, 32), fx(FM, 2)))
        if r == 0:
            tt(A("d1", 2, 3 * C, 3), A("win", 1, 3 * C, 3), A("win", 2, 3 * C, 3), ADD)
            act(A("d1", 1, 3 * C, 3), A("d1", 2, 3 * C, 3), Copy, 0.5)
        if r == 2:
            act(A("ec", 0, 112), I(WIN, fx(FE, 7)), Copy, 1.0 / 6.0)
            act(A("oc2", 0, 112), I(WIN, fx(FO, 7)), Copy, 1.0 / 6.0)
        tr(A("rw2", 0, C), A("pr2", 0, C))
        meeting(A("rw2", 0, C), "ml2", "gk2", "tk2")
        state(A("kk", 0, 32), I(A("tk2", 0, 512), fx(FK, 2)))
        if r == 0:
            tt(A("d1", 0, 3 * C, 3), A("win", 1, 3 * C, 3), A("d1", 1, 3 * C, 3), SUB)
        if r == 1:
            tt(A("d1", 0, 3 * C, 3), A("d1", 0, 3 * C, 3), A("d0", 1, 3 * C, 3), MUL)
        if r == 2:
            tt(A("sc", 0, 112), A("ec", 0, 112), A("oc2", 0, 112), ADD)
            tt(A("dc", 0, 112), A("ec", 0, 112), A("oc2", 0, 112), SUB)
            act(A("mmc", 0, 112), A("sc", 0, 112), Copy, 0.5, -0.5)
            act(A("ddc", 0, 112), A("dc", 0, 112), Copy, 0.5)
            quant("vvq", "vvs", 0, 128, "vt")
        for k, (c0, c1) in enumerate(VP):
            for b in range(4):
                mm(4 * ((k + 1) % 2) + b, "eq%d" % b, "es%d" % b, 0, lq, ls, c0, c1)
            for b in range(4):
                o, i1 = A("da%d" % b, c0, c1), P(4 * ((k + 1) % 2) + b, c1 - c0)
                if k == len(VP) - 1 and b % 2 == 1:
                    cp(o, i1)
                else:
                    act(o, i1)
        Y, yq, ys = "x%d" % (r + 1), "xq%d" % (r + 1), "xs%d" % (r + 1)
        outs = 8 + 6 * len(XP)
        for k, (c0, c1) in enumerate(XP):
            for b in range(4):
                tt(A(Y, 4 * c0 + b, 4 * c1, 4), I(A("da%d" % b, 0, C), A("kk", c0 // 16, c1 // 16)), A("vm", 4 * c0 + b, 4 * c1, 4), ADD)
            quant(yq, ys, c0, c1, Y)
            scores(r + 1, k)
            if r < 2 and k < last:
                for o, i1 in halves(r + 1, k):
                    act(o, i1, Copy, 0.5)
            if r == 2:
                mm(2 * k, "vvq", "vvs", 0, yq, ys, c0, c1)
                act(A("yb", c0, c1), P(2 * k, c1 - c0))
                move("y", (T["oc"][:, 4 * c0:4 * c1], [("oc", 0, 128, c0, c1, 1, 0)]), K(yq, c0, c1), "outs", outs)
                for q in range(4):
                    move("y", (T["osc"][4 * q:4 * q + 4, c0:c1], [("osc", 4 * q, 4 * q + 4, c0, c1, 1, 0)]), A(ys, c0, c1, 1, 32 * q, 32 * q + 4), "outs", outs)
                move("y", (T["y"][:, c0:c1], [("y", 0, 128, c0, c1, 1, 0)]), A("yb", c0, c1), "outs", outs)
    tt(A("dd3", 0, 112), I(A("d0", 0, 3 * C), fx(FE, 7)), A("ddc", 0, 112), MUL)
    tt(A("lrb", 0, 224, 2), A("mmc", 0, 112), A("dd3", 0, 112), ADD)
    tt(A("lrb", 1, 224, 2), A("mmc", 0, 112), A("dd3", 0, 112), SUB)
    for q in range(8):
        move("s" if q % 2 else "y", (T["lr"][:, 224 * q:224 * q + 224], [("lr", 0, 8, 224 * q, 224 * q + 224, 1, 0)]), A("lrb", 0, 224, 1, 16 * q + 8, 16 * q + 16), "outs", outs)
    for sem in ("sv", "ss", "st", "sg", "sent", "outs"):
        if F["clock"]["g"].get(sem, 0) < F["count"][sem]:
            g.wait_ge(T.sem[sem], F["count"][sem])
